import numpy as np
import ml_dtypes


def mxq(x, axis, fmt="e4m3"):
    dtype, down = {"e4m3": (ml_dtypes.float8_e4m3fn, 7), "e5m2": (ml_dtypes.float8_e5m2, 14)}[fmt]
    v = np.moveaxis(np.asarray(x, np.float32).astype(ml_dtypes.bfloat16).astype(np.float64), axis, -1)
    blocks = v.reshape(v.shape[:-1] + (-1, 32))
    amax = np.abs(blocks).max(-1, keepdims=True)
    byte = np.maximum(np.where(amax > 0, np.frexp(amax)[1] - 1 + 127, 0) - down, 1)
    scale = np.exp2(byte - 127.0)
    codes = (blocks / scale).astype(np.float32).astype(dtype).astype(np.float64)
    return np.moveaxis((codes * scale).reshape(v.shape), -1, axis)


WIDE = False


def mx_kscale(k):
    if not WIDE:
        return np.ones(k)
    levels = np.array([10, -10, 5, -5, 0])
    if k % 512:
        return np.exp2(np.random.permutation(np.resize(levels, k // 32))).repeat(32)
    a = np.empty((k // 512, 16))
    for p in range(k // 512):
        a[p, :8] = np.random.permutation(np.resize(levels, 8))
        for g in range(8):
            far = levels[np.abs(levels - a[p, g]) >= 10]
            a[p, g + 8] = far[np.random.randint(len(far))]
    return np.exp2(a.ravel()).repeat(32)


def f64(x):
    return np.asarray(x).astype(np.float64)


def striped(idx):
    return np.tile(idx.reshape(-1, 16).T, (8, 1)).astype(np.uint16)


def unstriped(offs):
    return offs[:16].T.reshape(-1).astype(np.int64)


def striped8(idx):
    return np.concatenate([x.reshape(-1, 16).T for x in idx]).astype(np.uint16)


def runs(offs, k):
    lists = np.stack([offs[16 * r : 16 * r + 16].T.reshape(-1) for r in range(8)]).astype(np.int64)
    return lists[np.arange(k) % 512 // 64]


def pack_weight(w):
    k, n = w.shape
    w = f64(np.asarray(w, np.float32).astype(ml_dtypes.bfloat16)).reshape(k // 32, 32, n)
    amax = np.abs(w).max(1)
    byte = np.clip(np.where(amax > 0, np.frexp(amax)[1] - 1 + 127 - 7, 1), 1, 254)
    scaled = (w * np.exp2(127.0 - byte)[:, None, :]).reshape(k, n).astype(np.float32)
    words = np.ascontiguousarray(scaled.reshape(k // 512, 128, 4, n).transpose(0, 1, 3, 2)).astype(ml_dtypes.float8_e4m3fn).view(np.uint8)
    return words, np.ascontiguousarray(byte.astype(np.uint8).reshape(k // 512, 16, n))


def unpack_weight(words, scales):
    g, p, n, _ = words.shape
    vals = np.ascontiguousarray(words).view(ml_dtypes.float8_e4m3fn).astype(np.float64) * np.repeat(np.exp2(scales.astype(np.float64) - 127.0), 8, axis=1)[..., None]
    return vals.transpose(0, 1, 3, 2).reshape(g * 512, n)


def relu(v):
    return np.maximum(v, 0.0)


K, T, S, V, N, H = 512, 2048, 512, 256, 512, 512


def setup_inputs():
    n = np.random.standard_normal
    s = mx_kscale(K)[:, None]
    u = mx_kscale(H)
    packed_xT = pack_weight(n((K, T)) * s)
    return {
        "x_words": packed_xT[0],
        "x_scales": packed_xT[1],
        "w1": (n((K, H)) / np.sqrt(K) / s).astype(np.float32),
        "w2": (n((K, H)) / np.sqrt(K) / s * u).astype(np.float32),
        "bg": (n((H, V)) * u[:, None]).astype(np.float32),
        "w3": (n((H, N)) / np.sqrt(H) / u[:, None]).astype(np.float32),
        "offs": striped(np.random.permutation(T)[:S]),
        "p1": striped8(np.stack([np.random.permutation(S)[:V] for _ in range(8)])),
        "p2": striped8(np.stack([np.random.permutation(S)[:V] for _ in range(8)])),
    }


def reference(x_words, x_scales, w1, w2, bg, w3, offs, p1, p2):
    xq = unpack_weight(x_words, x_scales)[:, unstriped(offs)]
    val = mxq(f64(w2), 0, "e4m3").T @ xq
    c1 = val[np.arange(H)[:, None], runs(p1, H)]
    s = relu(mxq(f64(w1), 0, "e4m3").T @ xq)
    s1 = np.exp(-1.0 * (s[np.arange(H)[:, None], runs(p1, H)]))
    c2 = val[np.arange(H)[:, None], runs(p2, H)]
    s2 = np.exp(-1.0 * (s[np.arange(H)[:, None], runs(p2, H)]))
    h = c2 + s2 * (f64(bg) - c2)
    z = c1 + s1 * (h - c1)
    return mxq(f64(w3), 0, "e4m3").T @ mxq(z, 0, "e4m3")

@@ -1,0 +1,192 @@
+from contextlib import ExitStack
+
+import concourse.mybir as mybir
+
+F32, BF16 = mybir.dt.float32, mybir.dt.bfloat16
+I32, U32, U16, U8 = mybir.dt.int32, mybir.dt.uint32, mybir.dt.uint16, mybir.dt.uint8
+FP8X4 = mybir.dt.float8_e4m3fn_x4
+ALU = mybir.AluOpType
+ACT = mybir.ActivationFunctionType
+
+K, T, S, V, N, H = 512, 2048, 512, 256, 512, 512
+P = 128
+PACK = 4
+FLOPS = 2 * (2 * K * H * S + H * N * V)
+
+ACT_GATHER = ((2,0),(2,1),(2,2),(2,3),(1,0),(1,1),(1,2),(1,3))
+W1_ACT = (1, 3)
+W2_ACT = ()
+
+
+def tile_picked_nerfvol_none_p_kernel(tc, x_words, x_scales, w1, w2, bg, w3, offs, p1, p2, out):
+    nc = tc.nc
+    with ExitStack() as ctx:
+        lists = ctx.enter_context(tc.tile_pool(name="lists", bufs=1))
+        sb = ctx.enter_context(tc.tile_pool(name="sb", bufs=1))
+        ps = ctx.enter_context(tc.psum_pool(name="ps", bufs=1))
+
+        def tile(name, shape, dtype, tag=None):
+            return sb.tile(shape, dtype, name=name, tag=tag or name, align_bytes=64)
+
+        def tiles(name, shape, dtype, count=PACK):
+            return [tile("%s%d" % (name, t), shape, dtype) for t in range(count)]
+
+        offs_t = lists.tile([P, S // 16], U16, name="offs_t")
+        p1_t = lists.tile([P, V // 16], U16, name="p1_t")
+        p2_t = lists.tile([P, V // 16], U16, name="p2_t")
+
+        scales = tile("scales", [P, T], U8)
+        w1_raw = tile("w1_raw", [P, PACK, H], F32, "w13")
+        zero_in = tile("zero_in", [P, 1], F32, "words")
+        zero_bias = tile("zero_bias", [P, 1], F32, "w2_raw")
+        one = tile("one", [P, 1], F32)
+
+        nc.vector.memset(scales[:].bitcast(I32), 0)
+        nc.vector.memset(zero_in[:], 0.0)
+        nc.vector.memset(zero_bias[:], 0.0)
+        nc.sync.dma_start(offs_t[:], offs)
+        nc.sync.dma_start(w1_raw[:], w1.rearrange("(p j) c -> p j c", j=PACK))
+        nc.sync.dma_start(p2_t[:], p2)
+        nc.sync.dma_start(p1_t[:], p1)
+        for q in range(4):
+            nc.sync.dma_start(scales[32 * q : 32 * q + 4, :].bitcast(I32), x_scales[0, 4 * q : 4 * q + 4, :].bitcast(I32))
+        nc.scalar.activation(one[:], zero_in[:], ACT.Exp, bias=zero_bias[:])
+        words = tile("words", [P, T], U32)
+        w2_raw = tile("w2_raw", [P, PACK, H], F32)
+        nc.sync.dma_start(words[:].bitcast(I32), x_words[0].rearrange("p n t -> p (n t)").bitcast(I32))
+        nc.sync.dma_start(w2_raw[:], w2.rearrange("(p j) c -> p j c", j=PACK))
+        bg_rows = bg.rearrange("(q t r) v -> t q r v", t=PACK, r=8)
+        w3_rows = w3.rearrange("(q t r) m -> t q r m", t=PACK, r=8)
+
+        def cast(on_act, dst, src):
+            if on_act:
+                nc.scalar.copy(dst, src)
+            else:
+                nc.vector.tensor_copy(dst, src)
+
+        def quantise_blocks(name, raw, on_act, after):
+            grouped = tiles(name + "_bf", [P, P * PACK], BF16)
+            codes = tiles(name + "_codes", [P, P], U32)
+            sc = tiles(name + "_sc", [P, P], U8)
+            cols = raw[:].rearrange("p j (q t r) -> p t q r j", t=PACK, r=8)
+
+            def round_block(t):
+                cast(t in on_act, grouped[t][:].rearrange("p (q r j) -> p q r j", r=8, j=PACK), cols[:, t])
+
+            def quantise(t):
+                nc.vector.quantize_mx(out=codes[t][:].bitcast(FP8X4), scales=sc[t][:], in_=grouped[t][:])
+                after(t, codes[t], sc[t])
+
+            round_block(0)
+            for t in range(1, PACK):
+                round_block(t)
+                quantise(t - 1)
+            quantise(PACK - 1)
+
+        x_codes = tile("x_codes", [P, S], U32)
+        x_bytes = tile("x_bytes", [P, S], U8)
+        s_ps = [ps.tile([P, S], F32, name="s_ps%d" % t) for t in range(PACK)]
+        val_ps = [ps.tile([P, S], F32, name="val_ps%d" % t) for t in range(PACK)]
+
+        def product(bank, codes, sc, cols):
+            nc.tensor.matmul_mx(out=bank[:, cols], lhsT=codes[:].bitcast(FP8X4), lhsT_scale=sc[:],
+                                rhs=x_codes[:, cols].bitcast(FP8X4), rhs_scale=x_bytes[:, cols], start=True, stop=True)
+
+        w1_q = []
+        quantise_blocks("w1", w1_raw, W1_ACT, lambda t, c, s: w1_q.append((c, s)))
+        nc.vector.tensor_copy(x_bytes[:], scales[:].indirect(offs_t[:]))
+        for half in range(2):
+            cols = slice(256 * half, 256 * (half + 1))
+            nc.vector.tensor_copy(x_codes[:, cols], words[:].indirect(offs_t[:, 16 * half : 16 * (half + 1)]))
+            for t in range(PACK):
+                product(s_ps[t], w1_q[t][0], w1_q[t][1], cols)
+
+        bg_all = tile("bg_all", [P, PACK, V], F32, "scales")
+        for t in range(PACK):
+            nc.sync.dma_start(bg_all[:, t, :], bg_rows[t])
+        w3_raw = tile("w3_raw", [P, PACK, N], F32, "words")
+        for t in range(PACK):
+            nc.sync.dma_start(w3_raw[:, t, :], w3_rows[t])
+
+        quantise_blocks("w2", w2_raw, W2_ACT, lambda t, c, s: product(val_ps[t], c, s, slice(0, S)))
+
+        dens = tiles("dens", [P, S], F32)
+        thru = tiles("thru", [P, S], F32)
+        emit = tiles("emit", [P, S], F32)
+        e1 = tiles("e1_", [P, V], F32)
+        e2 = tiles("e2_", [P, V], F32)
+        seen_bg = tiles("seen_bg", [P, V], F32)
+        behind = tiles("behind", [P, V], F32)
+        seen_behind = tiles("seen_behind", [P, V], F32)
+        z_neg = tile("z_neg", [P, PACK, V], F32)
+        w3_bf = tiles("w3_bf", [P, N * PACK // 2], BF16, 2)
+        w3_codes = tiles("w3_codes", [P, N // 2], U32, 2)
+        w3_sc = tiles("w3_sc", [P, N // 2], U8, 2)
+
+        def density(t):
+            nc.scalar.activation(dens[t][:], s_ps[t][:], ACT.Relu)
+            nc.scalar.activation(thru[t][:], dens[t][:], ACT.Exp, scale=-1.0)
+
+        def fetch(which, t):
+            if (which, t) in ACT_GATHER:
+                dst, lst = (e1, p1_t) if which == 1 else (e2, p2_t)
+                nc.scalar.activation(dst[t][:], dens[t][:].indirect(lst[:]), ACT.Exp, scale=-1.0)
+
+        def emission(t):
+            nc.vector.scalar_tensor_tensor(emit[t][:], thru[t][:], one[:], val_ps[t][:], ALU.subtract, ALU.mult)
+
+        def dim(which, t):
+            dst, src, got, lst = (seen_behind[t][:], behind[t][:], e1, p1_t) if which == 1 else (seen_bg[t][:], bg_all[:, t, :], e2, p2_t)
+            if (which, t) in ACT_GATHER:
+                nc.vector.tensor_tensor(dst, got[t][:], src, ALU.mult)
+            else:
+                nc.vector.tensor_tensor(dst, thru[t][:].indirect(lst[:]), src, ALU.mult)
+
+        def far_sample(t):
+            nc.vector.tensor_tensor(behind[t][:], emit[t][:].indirect(p2_t[:]), seen_bg[t][:], ALU.subtract)
+
+        def near_sample(t):
+            nc.vector.tensor_tensor(z_neg[:, t, :], emit[t][:].indirect(p1_t[:]), seen_behind[t][:], ALU.add)
+
+        def w3_quantise(u):
+            nc.vector.quantize_mx(out=w3_codes[u][:].bitcast(FP8X4), scales=w3_sc[u][:], in_=w3_bf[u][:])
+
+        for t in range(PACK):
+            density(t)
+            if t > 0:
+                fetch(1, t - 1)
+            fetch(2, t)
+        fetch(1, PACK - 1)
+        for u in range(2):
+            nc.scalar.copy(w3_bf[u][:].rearrange("p (m t) -> p m t", t=PACK), w3_raw[:, :, 256 * u : 256 * (u + 1)].rearrange("p t m -> p m t"))
+
+        emission(0)
+        dim(2, 0)
+        far_sample(0)
+        for t in range(1, PACK):
+            emission(t)
+            dim(1, t - 1)
+            dim(2, t)
+            near_sample(t - 1)
+            far_sample(t)
+        w3_quantise(0)
+        dim(1, PACK - 1)
+        w3_quantise(1)
+        near_sample(PACK - 1)
+
+        z_bf = tile("z_bf", [P, V * PACK], BF16)
+        z_codes = tile("z_codes", [P, V], U32)
+        z_sc = tile("z_sc", [P, V], U8)
+        nc.vector.tensor_scalar(z_bf[:].rearrange("p (v t) -> p v t", t=PACK), z_neg[:].rearrange("p t v -> p v t"), -1.0, None, ALU.mult)
+        nc.vector.quantize_mx(out=z_codes[:].bitcast(FP8X4), scales=z_sc[:], in_=z_bf[:])
+
+        res = tiles("res", [P, 2, V], F32, 2)
+        out_rows = out.rearrange("(h u p) v -> h p u v", u=2, p=P)
+        for u in range(PACK):
+            acc = ps.tile([P, V], F32, name="s_ps%d" % u)
+            cs = slice(P * (u % 2), P * (u % 2 + 1))
+            nc.tensor.matmul_mx(out=acc[:], lhsT=w3_codes[u // 2][:, cs].bitcast(FP8X4), lhsT_scale=w3_sc[u // 2][:, cs],
+                                rhs=z_codes[:].bitcast(FP8X4), rhs_scale=z_sc[:], start=True, stop=True)
+            cast(u % 2 == 0, res[u // 2][:, u % 2, :], acc[:])
+            if u % 2 == 1:
+                nc.sync.dma_start(out_rows[u // 2], res[u // 2][:])

@@ -13,16 +13,13 @@ P = 128
 PACK = 4
 FLOPS = 2 * (2 * K * H * S + H * N * V)
 
-ACT_GATHER = ((2,0),(2,1),(2,2),(2,3),(1,0),(1,1),(1,2),(1,3))
-W1_ACT = (1, 3)
-W2_ACT = ()
-
 
 def tile_picked_nerfvol_none_p_kernel(tc, x_words, x_scales, w1, w2, bg, w3, offs, p1, p2, out):
     nc = tc.nc
     with ExitStack() as ctx:
         lists = ctx.enter_context(tc.tile_pool(name="lists", bufs=1))
         sb = ctx.enter_context(tc.tile_pool(name="sb", bufs=1))
+        shared = ctx.enter_context(tc.tile_pool(name="shared", bufs=1))
         ps = ctx.enter_context(tc.psum_pool(name="ps", bufs=1))
 
         def tile(name, shape, dtype, tag=None):
@@ -35,28 +32,28 @@ def tile_picked_nerfvol_none_p_kernel(tc, x_words, x_scales, w1, w2, bg, w3, off
         p1_t = lists.tile([P, V // 16], U16, name="p1_t")
         p2_t = lists.tile([P, V // 16], U16, name="p2_t")
 
-        scales = tile("scales", [P, T], U8)
-        w1_raw = tile("w1_raw", [P, PACK, H], F32, "w13")
+        scales = shared.tile([P, T], U8, name="scales", offset=0, align_bytes=64)
+        w2_raw = tile("w2_raw", [P, PACK, H], F32)
         zero_in = tile("zero_in", [P, 1], F32, "words")
-        zero_bias = tile("zero_bias", [P, 1], F32, "w2_raw")
+        zero_bias = tile("zero_bias", [P, 1], F32, "w1_raw")
         one = tile("one", [P, 1], F32)
 
         nc.vector.memset(scales[:].bitcast(I32), 0)
         nc.vector.memset(zero_in[:], 0.0)
         nc.vector.memset(zero_bias[:], 0.0)
         nc.sync.dma_start(offs_t[:], offs)
-        nc.sync.dma_start(w1_raw[:], w1.rearrange("(p j) c -> p j c", j=PACK))
+        nc.sync.dma_start(w2_raw[:], w2.rearrange("(p j) c -> p j c", j=PACK))
         nc.sync.dma_start(p2_t[:], p2)
         nc.sync.dma_start(p1_t[:], p1)
         for q in range(4):
             nc.sync.dma_start(scales[32 * q : 32 * q + 4, :].bitcast(I32), x_scales[0, 4 * q : 4 * q + 4, :].bitcast(I32))
         nc.scalar.activation(one[:], zero_in[:], ACT.Exp, bias=zero_bias[:])
         words = tile("words", [P, T], U32)
-        w2_raw = tile("w2_raw", [P, PACK, H], F32)
+        w1_raw = tile("w1_raw", [P, PACK, H], F32)
         nc.sync.dma_start(words[:].bitcast(I32), x_words[0].rearrange("p n t -> p (n t)").bitcast(I32))
-        nc.sync.dma_start(w2_raw[:], w2.rearrange("(p j) c -> p j c", j=PACK))
-        bg_rows = bg.rearrange("(q t r) v -> t q r v", t=PACK, r=8)
-        w3_rows = w3.rearrange("(q t r) m -> t q r m", t=PACK, r=8)
+        nc.sync.dma_start(w1_raw[:], w1.rearrange("(p j) c -> p j c", j=PACK))
+        bg_rows = bg.rearrange("(a t r) v -> t a r v", t=PACK, r=4)
+        w3_rows = w3.rearrange("(a t r) m -> t a r m", t=PACK, r=4)
 
         def cast(on_act, dst, src):
             if on_act:
@@ -64,26 +61,17 @@ def tile_picked_nerfvol_none_p_kernel(tc, x_words, x_scales, w1, w2, bg, w3, off
             else:
                 nc.vector.tensor_copy(dst, src)
 
-        def quantise_blocks(name, raw, on_act, after):
-            grouped = tiles(name + "_bf", [P, P * PACK], BF16)
-            codes = tiles(name + "_codes", [P, P], U32)
-            sc = tiles(name + "_sc", [P, P], U8)
-            cols = raw[:].rearrange("p j (q t r) -> p t q r j", t=PACK, r=8)
+        def weave(dst, src):
+            return dst.rearrange("p (c i t) -> p c t i", i=4, t=PACK), src.rearrange("p t (c i) -> p c t i", i=4)
 
-            def round_block(t):
-                cast(t in on_act, grouped[t][:].rearrange("p (q r j) -> p q r j", r=8, j=PACK), cols[:, t])
+        def round_block(on_act, grouped, raw, t):
+            cols = raw[:].rearrange("p j (a t i) -> p t a j i", t=PACK, i=4)
+            cast(on_act, grouped[:].rearrange("p (a i j) -> p a j i", i=4, j=PACK), cols[:, t])
 
-            def quantise(t):
-                nc.vector.quantize_mx(out=codes[t][:].bitcast(FP8X4), scales=sc[t][:], in_=grouped[t][:])
-                after(t, codes[t], sc[t])
+        def quantise(codes, sc, grouped):
+            nc.vector.quantize_mx(out=codes[:].bitcast(FP8X4), scales=sc[:], in_=grouped[:])
 
-            round_block(0)
-            for t in range(1, PACK):
-                round_block(t)
-                quantise(t - 1)
-            quantise(PACK - 1)
-
-        x_codes = tile("x_codes", [P, S], U32)
+        x_codes = shared.tile([P, S], U32, name="x_codes", offset=512, align_bytes=64)
         x_bytes = tile("x_bytes", [P, S], U8)
         s_ps = [ps.tile([P, S], F32, name="s_ps%d" % t) for t in range(PACK)]
         val_ps = [ps.tile([P, S], F32, name="val_ps%d" % t) for t in range(PACK)]
@@ -92,101 +80,126 @@ def tile_picked_nerfvol_none_p_kernel(tc, x_words, x_scales, w1, w2, bg, w3, off
             nc.tensor.matmul_mx(out=bank[:, cols], lhsT=codes[:].bitcast(FP8X4), lhsT_scale=sc[:],
                                 rhs=x_codes[:, cols].bitcast(FP8X4), rhs_scale=x_bytes[:, cols], start=True, stop=True)
 
-        w1_q = []
-        quantise_blocks("w1", w1_raw, W1_ACT, lambda t, c, s: w1_q.append((c, s)))
         nc.vector.tensor_copy(x_bytes[:], scales[:].indirect(offs_t[:]))
+        w2_bf = tiles("w2_bf", [P, P * PACK], BF16)
+        w2_codes = tiles("w2_codes", [P, P], U32)
+        w2_sc = [shared.tile([P, P], U8, name="w2_sc%d" % t, offset=P * t, align_bytes=64) for t in range(PACK)]
+        for t in range(PACK):
+            round_block(True, w2_bf[t], w2_raw, t)
+            quantise(w2_codes[t], w2_sc[t], w2_bf[t])
         for half in range(2):
-            cols = slice(256 * half, 256 * (half + 1))
-            nc.vector.tensor_copy(x_codes[:, cols], words[:].indirect(offs_t[:, 16 * half : 16 * (half + 1)]))
-            for t in range(PACK):
-                product(s_ps[t], w1_q[t][0], w1_q[t][1], cols)
+            nc.vector.tensor_copy(x_codes[:, 256 * half : 256 * (half + 1)], words[:].indirect(offs_t[:, 16 * half : 16 * (half + 1)]))
+        for t in range(PACK):
+            for half in range(2):
+                product(val_ps[t], w2_codes[t], w2_sc[t], slice(256 * half, 256 * (half + 1)))
 
-        bg_all = tile("bg_all", [P, PACK, V], F32, "scales")
+        bg_all = tile("bg_all", [P, PACK, V], F32, "w2_raw")
         for t in range(PACK):
             nc.sync.dma_start(bg_all[:, t, :], bg_rows[t])
         w3_raw = tile("w3_raw", [P, PACK, N], F32, "words")
         for t in range(PACK):
             nc.sync.dma_start(w3_raw[:, t, :], w3_rows[t])
 
-        quantise_blocks("w2", w2_raw, W2_ACT, lambda t, c, s: product(val_ps[t], c, s, slice(0, S)))
+        w1_bf = tile("w1_bf", [P, H * PACK], BF16)
+        w1_codes = tile("w1_codes", [P, H], U32)
+        w1_sc = tile("w1_sc", [P, H], U8)
 
+        def w1_round(ts, js):
+            dst = w1_bf[:].rearrange("p (t a i j) -> p a t j i", t=PACK, i=4, j=PACK)
+            src = w1_raw[:].rearrange("p j (a t i) -> p a t j i", t=PACK, i=4)
+            nc.vector.tensor_copy(dst[:, :, ts, js, :], src[:, :, ts, js, :])
+
+        def w1_quantise(t0, t1):
+            quantise(w1_codes[:, P * t0 : P * t1], w1_sc[:, P * t0 : P * t1], w1_bf[:, P * PACK * t0 : P * PACK * t1])
+            for t in range(t0, t1):
+                product(s_ps[t], w1_codes[:, P * t : P * (t + 1)], w1_sc[:, P * t : P * (t + 1)], slice(0, S))
+
+        val = tiles("val", [P, S], F32)
         dens = tiles("dens", [P, S], F32)
-        thru = tiles("thru", [P, S], F32)
-        emit = tiles("emit", [P, S], F32)
         e1 = tiles("e1_", [P, V], F32)
         e2 = tiles("e2_", [P, V], F32)
-        seen_bg = tiles("seen_bg", [P, V], F32)
-        behind = tiles("behind", [P, V], F32)
-        seen_behind = tiles("seen_behind", [P, V], F32)
-        z_neg = tile("z_neg", [P, PACK, V], F32)
-        w3_bf = tiles("w3_bf", [P, N * PACK // 2], BF16, 2)
+        d1 = tiles("d1_", [P, V], F32)
+        d2 = tiles("d2_", [P, V], F32)
+        u2 = tiles("u2_", [P, V], F32)
+        u1 = tile("u1", [P, PACK, V], F32)
+        behind = tile("behind", [P, PACK, V], F32)
+        w3_bf = [tile("w3_bf%d" % u, [P, N * PACK // 2], BF16, "dens%d" % u) for u in range(2)]
         w3_codes = tiles("w3_codes", [P, N // 2], U32, 2)
         w3_sc = tiles("w3_sc", [P, N // 2], U8, 2)
 
+        def fetch(dst, lst, t):
+            nc.scalar.activation(dst[t][:], dens[t][:].indirect(lst[:]), ACT.Exp, scale=-1.0)
+
+        def far_contrast(t):
+            nc.vector.tensor_tensor(d2[t][:], val[t][:].indirect(p2_t[:]), bg_all[:, t, :], ALU.subtract)
+
+        def far_share(t):
+            nc.vector.scalar_tensor_tensor(u2[t][:], e2[t][:], one[:], d2[t][:], ALU.subtract, ALU.mult)
+
+        def far_blend(t):
+            nc.vector.tensor_tensor(behind[:, t, :], bg_all[:, t, :], u2[t][:], ALU.subtract)
+
+        def near_contrast(t):
+            nc.vector.tensor_tensor(d1[t][:], val[t][:].indirect(p1_t[:]), behind[:, t, :], ALU.subtract)
+
+        def near_share(t):
+            nc.vector.scalar_tensor_tensor(u1[:, t, :], e1[t][:], one[:], d1[t][:], ALU.subtract, ALU.mult)
+
         def density(t):
             nc.scalar.activation(dens[t][:], s_ps[t][:], ACT.Relu)
-            nc.scalar.activation(thru[t][:], dens[t][:], ACT.Exp, scale=-1.0)
-
-        def fetch(which, t):
-            if (which, t) in ACT_GATHER:
-                dst, lst = (e1, p1_t) if which == 1 else (e2, p2_t)
-                nc.scalar.activation(dst[t][:], dens[t][:].indirect(lst[:]), ACT.Exp, scale=-1.0)
-
-        def emission(t):
-            nc.vector.scalar_tensor_tensor(emit[t][:], thru[t][:], one[:], val_ps[t][:], ALU.subtract, ALU.mult)
-
-        def dim(which, t):
-            dst, src, got, lst = (seen_behind[t][:], behind[t][:], e1, p1_t) if which == 1 else (seen_bg[t][:], bg_all[:, t, :], e2, p2_t)
-            if (which, t) in ACT_GATHER:
-                nc.vector.tensor_tensor(dst, got[t][:], src, ALU.mult)
-            else:
-                nc.vector.tensor_tensor(dst, thru[t][:].indirect(lst[:]), src, ALU.mult)
-
-        def far_sample(t):
-            nc.vector.tensor_tensor(behind[t][:], emit[t][:].indirect(p2_t[:]), seen_bg[t][:], ALU.subtract)
-
-        def near_sample(t):
-            nc.vector.tensor_tensor(z_neg[:, t, :], emit[t][:].indirect(p1_t[:]), seen_behind[t][:], ALU.add)
-
-        def w3_quantise(u):
-            nc.vector.quantize_mx(out=w3_codes[u][:].bitcast(FP8X4), scales=w3_sc[u][:], in_=w3_bf[u][:])
 
         for t in range(PACK):
-            density(t)
-            if t > 0:
-                fetch(1, t - 1)
-            fetch(2, t)
-        fetch(1, PACK - 1)
-        for u in range(2):
-            nc.scalar.copy(w3_bf[u][:].rearrange("p (m t) -> p m t", t=PACK), w3_raw[:, :, 256 * u : 256 * (u + 1)].rearrange("p t m -> p m t"))
-
-        emission(0)
-        dim(2, 0)
-        far_sample(0)
+            nc.scalar.copy(val[t][:], val_ps[t][:])
+        whole = slice(0, PACK)
+        w1_round(slice(0, 1), whole)
+        w1_round(slice(1, 2), whole)
+        w1_quantise(0, 1)
+        w1_round(slice(2, 4), whole)
+        w1_quantise(1, 2)
+        far_contrast(0)
+        w1_quantise(2, 4)
         for t in range(1, PACK):
-            emission(t)
-            dim(1, t - 1)
-            dim(2, t)
-            near_sample(t - 1)
-            far_sample(t)
-        w3_quantise(0)
-        dim(1, PACK - 1)
-        w3_quantise(1)
-        near_sample(PACK - 1)
+            far_contrast(t)
 
-        z_bf = tile("z_bf", [P, V * PACK], BF16)
-        z_codes = tile("z_codes", [P, V], U32)
-        z_sc = tile("z_sc", [P, V], U8)
-        nc.vector.tensor_scalar(z_bf[:].rearrange("p (v t) -> p v t", t=PACK), z_neg[:].rearrange("p t v -> p v t"), -1.0, None, ALU.mult)
-        nc.vector.quantize_mx(out=z_codes[:].bitcast(FP8X4), scales=z_sc[:], in_=z_bf[:])
+        pairs = ((0, 1), (2, 3))
+        for pair in pairs:
+            for t in pair:
+                density(t)
+            for t in pair:
+                fetch(e2, p2_t, t)
+        for t in range(PACK):
+            fetch(e1, p1_t, t)
+        for u in range(2):
+            nc.scalar.copy(*weave(w3_bf[u][:], w3_raw[:, :, 256 * u : 256 * (u + 1)]))
 
-        res = tiles("res", [P, 2, V], F32, 2)
-        out_rows = out.rearrange("(h u p) v -> h p u v", u=2, p=P)
-        for u in range(PACK):
-            acc = ps.tile([P, V], F32, name="s_ps%d" % u)
-            cs = slice(P * (u % 2), P * (u % 2 + 1))
-            nc.tensor.matmul_mx(out=acc[:], lhsT=w3_codes[u // 2][:, cs].bitcast(FP8X4), lhsT_scale=w3_sc[u // 2][:, cs],
-                                rhs=z_codes[:].bitcast(FP8X4), rhs_scale=z_sc[:], start=True, stop=True)
-            cast(u % 2 == 0, res[u // 2][:, u % 2, :], acc[:])
-            if u % 2 == 1:
-                nc.sync.dma_start(out_rows[u // 2], res[u // 2][:])
+        for pair in pairs:
+            for step in (far_share, far_blend, near_contrast):
+                for t in pair:
+                    step(t)
+        for t in range(PACK):
+            near_share(t)
+        quantise(w3_codes[0], w3_sc[0], w3_bf[0])
+
+        HV = V // 2
+        z_bf = tiles("z_bf", [P, HV * PACK], BF16, 2)
+        z_codes = tiles("z_codes", [P, HV], U32, 2)
+        z_sc = tiles("z_sc", [P, HV], U8, 2)
+        halves = [slice(0, HV), slice(HV, V)]
+        for h in range(2):
+            dst, src0 = weave(z_bf[h][:], behind[:, :, halves[h]])
+            dst, src1 = weave(z_bf[h][:], u1[:, :, halves[h]])
+            nc.vector.tensor_tensor(dst, src0, src1, ALU.subtract)
+        quantise(z_codes[0], z_sc[0], z_bf[0])
+        quantise(w3_codes[1], w3_sc[1], w3_bf[1])
+        quantise(z_codes[1], z_sc[1], z_bf[1])
+        out_rows = out.rearrange("(u p) v -> p u v", p=P)
+        for h in range(2):
+            for g in range(2):
+                acc = ps.tile([P, 2, HV], F32, name="val_ps%d" % (2 * h + g))
+                res = tile("res%d%d" % (h, g), [P, 2, HV], F32)
+                for u in range(2):
+                    cs = slice(P * u, P * (u + 1))
+                    nc.tensor.matmul_mx(out=acc[:, u, :], lhsT=w3_codes[g][:, cs].bitcast(FP8X4), lhsT_scale=w3_sc[g][:, cs],
+                                        rhs=z_codes[h][:].bitcast(FP8X4), rhs_scale=z_sc[h][:], start=True, stop=True)
+                cast(g == 0, res[:], acc[:])
+                nc.sync.dma_start(out_rows[:, 2 * g : 2 * g + 2, halves[h]], res[:])

@@ -11,7 +11,15 @@ ACT = mybir.ActivationFunctionType
 K, T, S, V, N, H = 512, 2048, 512, 256, 512, 512
 P = 128
 PACK = 4
+RUN = 4
+GROUP = 16
+QUADRANT = 32
+SCALE_ROWS = 4
 FLOPS = 2 * (2 * K * H * S + H * N * V)
+
+
+def halves(n):
+    return slice(0, n // 2), slice(n // 2, n)
 
 
 def tile_picked_nerfvol_none_p_kernel(tc, x_words, x_scales, w1, w2, bg, w3, offs, p1, p2, out):
@@ -26,11 +34,17 @@ def tile_picked_nerfvol_none_p_kernel(tc, x_words, x_scales, w1, w2, bg, w3, off
             return sb.tile(shape, dtype, name=name, tag=tag or name, align_bytes=64)
 
         def tiles(name, shape, dtype, count=PACK):
-            return [tile("%s%d" % (name, t), shape, dtype) for t in range(count)]
+            return [tile("%s%d" % (name, n), shape, dtype) for n in range(count)]
 
-        offs_t = lists.tile([P, S // 16], U16, name="offs_t")
-        p1_t = lists.tile([P, V // 16], U16, name="p1_t")
-        p2_t = lists.tile([P, V // 16], U16, name="p2_t")
+        def weave(dst, src):
+            return dst.rearrange("p (c i t) -> p c t i", i=RUN, t=PACK), src.rearrange("p t (c i) -> p c t i", i=RUN)
+
+        def quantise(codes, scale_bytes, rounded):
+            nc.vector.quantize_mx(out=codes[:].bitcast(FP8X4), scales=scale_bytes[:], in_=rounded[:])
+
+        offs_t = lists.tile([P, S // GROUP], U16, name="offs_t")
+        p1_t = lists.tile([P, V // GROUP], U16, name="p1_t")
+        p2_t = lists.tile([P, V // GROUP], U16, name="p2_t")
 
         scales = shared.tile([P, T], U8, name="scales", offset=0, align_bytes=64)
         w2_raw = tile("w2_raw", [P, PACK, H], F32)
@@ -45,54 +59,46 @@ def tile_picked_nerfvol_none_p_kernel(tc, x_words, x_scales, w1, w2, bg, w3, off
         nc.sync.dma_start(w2_raw[:], w2.rearrange("(p j) c -> p j c", j=PACK))
         nc.sync.dma_start(p2_t[:], p2)
         nc.sync.dma_start(p1_t[:], p1)
-        for q in range(4):
-            nc.sync.dma_start(scales[32 * q : 32 * q + 4, :].bitcast(I32), x_scales[0, 4 * q : 4 * q + 4, :].bitcast(I32))
+        for r in range(SCALE_ROWS):
+            nc.sync.dma_start(scales[r:P:QUADRANT, :].bitcast(I32), x_scales[0, r : K // QUADRANT : SCALE_ROWS, :].bitcast(I32))
         nc.scalar.activation(one[:], zero_in[:], ACT.Exp, bias=zero_bias[:])
         words = tile("words", [P, T], U32)
         w1_raw = tile("w1_raw", [P, PACK, H], F32)
-        nc.sync.dma_start(words[:].bitcast(I32), x_words[0].rearrange("p n t -> p (n t)").bitcast(I32))
+        nc.sync.dma_start(words[:].bitcast(I32), x_words[0].rearrange("p n j -> p (n j)").bitcast(I32))
         nc.sync.dma_start(w1_raw[:], w1.rearrange("(p j) c -> p j c", j=PACK))
-        bg_rows = bg.rearrange("(a t r) v -> t a r v", t=PACK, r=4)
-        w3_rows = w3.rearrange("(a t r) m -> t a r m", t=PACK, r=4)
 
-        def cast(on_act, dst, src):
-            if on_act:
-                nc.scalar.copy(dst, src)
-            else:
-                nc.vector.tensor_copy(dst, src)
-
-        def weave(dst, src):
-            return dst.rearrange("p (c i t) -> p c t i", i=4, t=PACK), src.rearrange("p t (c i) -> p c t i", i=4)
-
-        def round_block(on_act, grouped, raw, t):
-            cols = raw[:].rearrange("p j (a t i) -> p t a j i", t=PACK, i=4)
-            cast(on_act, grouped[:].rearrange("p (a i j) -> p a j i", i=4, j=PACK), cols[:, t])
-
-        def quantise(codes, sc, grouped):
-            nc.vector.quantize_mx(out=codes[:].bitcast(FP8X4), scales=sc[:], in_=grouped[:])
-
-        x_codes = shared.tile([P, S], U32, name="x_codes", offset=512, align_bytes=64)
+        x_codes = shared.tile([P, S], U32, name="x_codes", offset=PACK * P, align_bytes=64)
         x_bytes = tile("x_bytes", [P, S], U8)
         s_ps = [ps.tile([P, S], F32, name="s_ps%d" % t) for t in range(PACK)]
         val_ps = [ps.tile([P, S], F32, name="val_ps%d" % t) for t in range(PACK)]
 
-        def product(bank, codes, sc, cols):
-            nc.tensor.matmul_mx(out=bank[:, cols], lhsT=codes[:].bitcast(FP8X4), lhsT_scale=sc[:],
-                                rhs=x_codes[:, cols].bitcast(FP8X4), rhs_scale=x_bytes[:, cols], start=True, stop=True)
+        def project(bank, codes, scale_bytes, samples):
+            nc.tensor.matmul_mx(
+                out=bank[:, samples],
+                lhsT=codes[:].bitcast(FP8X4),
+                lhsT_scale=scale_bytes[:],
+                rhs=x_codes[:, samples].bitcast(FP8X4),
+                rhs_scale=x_bytes[:, samples],
+                start=True,
+                stop=True,
+            )
 
         nc.vector.tensor_copy(x_bytes[:], scales[:].indirect(offs_t[:]))
         w2_bf = tiles("w2_bf", [P, P * PACK], BF16)
         w2_codes = tiles("w2_codes", [P, P], U32)
         w2_sc = [shared.tile([P, P], U8, name="w2_sc%d" % t, offset=P * t, align_bytes=64) for t in range(PACK)]
+        w2_cols = w2_raw[:].rearrange("p j (a t r) -> p t a j r", t=PACK, r=RUN)
         for t in range(PACK):
-            round_block(True, w2_bf[t], w2_raw, t)
+            nc.scalar.copy(w2_bf[t][:].rearrange("p (a r j) -> p a j r", r=RUN, j=PACK), w2_cols[:, t])
             quantise(w2_codes[t], w2_sc[t], w2_bf[t])
-        for half in range(2):
-            nc.vector.tensor_copy(x_codes[:, 256 * half : 256 * (half + 1)], words[:].indirect(offs_t[:, 16 * half : 16 * (half + 1)]))
+        for samples, entries in zip(halves(S), halves(S // GROUP)):
+            nc.vector.tensor_copy(x_codes[:, samples], words[:].indirect(offs_t[:, entries]))
         for t in range(PACK):
-            for half in range(2):
-                product(val_ps[t], w2_codes[t], w2_sc[t], slice(256 * half, 256 * (half + 1)))
+            for samples in halves(S):
+                project(val_ps[t], w2_codes[t], w2_sc[t], samples)
 
+        bg_rows = bg.rearrange("(a t r) v -> t a r v", t=PACK, r=RUN)
+        w3_rows = w3.rearrange("(a t r) m -> t a r m", t=PACK, r=RUN)
         bg_all = tile("bg_all", [P, PACK, V], F32, "w2_raw")
         for t in range(PACK):
             nc.sync.dma_start(bg_all[:, t, :], bg_rows[t])
@@ -103,17 +109,6 @@ def tile_picked_nerfvol_none_p_kernel(tc, x_words, x_scales, w1, w2, bg, w3, off
         w1_bf = tile("w1_bf", [P, H * PACK], BF16)
         w1_codes = tile("w1_codes", [P, H], U32)
         w1_sc = tile("w1_sc", [P, H], U8)
-
-        def w1_round(ts, js):
-            dst = w1_bf[:].rearrange("p (t a i j) -> p a t j i", t=PACK, i=4, j=PACK)
-            src = w1_raw[:].rearrange("p j (a t i) -> p a t j i", t=PACK, i=4)
-            nc.vector.tensor_copy(dst[:, :, ts, js, :], src[:, :, ts, js, :])
-
-        def w1_quantise(t0, t1):
-            quantise(w1_codes[:, P * t0 : P * t1], w1_sc[:, P * t0 : P * t1], w1_bf[:, P * PACK * t0 : P * PACK * t1])
-            for t in range(t0, t1):
-                product(s_ps[t], w1_codes[:, P * t : P * (t + 1)], w1_sc[:, P * t : P * (t + 1)], slice(0, S))
-
         val = tiles("val", [P, S], F32)
         dens = tiles("dens", [P, S], F32)
         e1 = tiles("e1_", [P, V], F32)
@@ -123,12 +118,25 @@ def tile_picked_nerfvol_none_p_kernel(tc, x_words, x_scales, w1, w2, bg, w3, off
         u2 = tiles("u2_", [P, V], F32)
         u1 = tile("u1", [P, PACK, V], F32)
         behind = tile("behind", [P, PACK, V], F32)
-        w3_bf = [tile("w3_bf%d" % u, [P, N * PACK // 2], BF16, "dens%d" % u) for u in range(2)]
+        w3_bf = [tile("w3_bf%d" % g, [P, N * PACK // 2], BF16, "dens%d" % g) for g in range(2)]
         w3_codes = tiles("w3_codes", [P, N // 2], U32, 2)
         w3_sc = tiles("w3_sc", [P, N // 2], U8, 2)
 
-        def fetch(dst, lst, t):
-            nc.scalar.activation(dst[t][:], dens[t][:].indirect(lst[:]), ACT.Exp, scale=-1.0)
+        def w1_round(t0, t1):
+            dst = w1_bf[:].rearrange("p (t a r j) -> p a t j r", t=PACK, r=RUN, j=PACK)
+            src = w1_raw[:].rearrange("p j (a t r) -> p a t j r", t=PACK, r=RUN)
+            nc.vector.tensor_copy(dst[:, :, t0:t1], src[:, :, t0:t1])
+
+        def w1_project(t0, t1):
+            quantise(w1_codes[:, P * t0 : P * t1], w1_sc[:, P * t0 : P * t1], w1_bf[:, P * PACK * t0 : P * PACK * t1])
+            for t in range(t0, t1):
+                project(s_ps[t], w1_codes[:, P * t : P * (t + 1)], w1_sc[:, P * t : P * (t + 1)], slice(0, S))
+
+        def density(t):
+            nc.scalar.activation(dens[t][:], s_ps[t][:], ACT.Relu)
+
+        def transmittance(e, list_t, t):
+            nc.scalar.activation(e[t][:], dens[t][:].indirect(list_t[:]), ACT.Exp, scale=-1.0)
 
         def far_contrast(t):
             nc.vector.tensor_tensor(d2[t][:], val[t][:].indirect(p2_t[:]), bg_all[:, t, :], ALU.subtract)
@@ -145,19 +153,15 @@ def tile_picked_nerfvol_none_p_kernel(tc, x_words, x_scales, w1, w2, bg, w3, off
         def near_share(t):
             nc.vector.scalar_tensor_tensor(u1[:, t, :], e1[t][:], one[:], d1[t][:], ALU.subtract, ALU.mult)
 
-        def density(t):
-            nc.scalar.activation(dens[t][:], s_ps[t][:], ACT.Relu)
-
         for t in range(PACK):
             nc.scalar.copy(val[t][:], val_ps[t][:])
-        whole = slice(0, PACK)
-        w1_round(slice(0, 1), whole)
-        w1_round(slice(1, 2), whole)
-        w1_quantise(0, 1)
-        w1_round(slice(2, 4), whole)
-        w1_quantise(1, 2)
+        w1_round(0, 1)
+        w1_round(1, 2)
+        w1_project(0, 1)
+        w1_project(1, 2)
+        w1_round(2, 4)
         far_contrast(0)
-        w1_quantise(2, 4)
+        w1_project(2, 4)
         for t in range(1, PACK):
             far_contrast(t)
 
@@ -166,11 +170,11 @@ def tile_picked_nerfvol_none_p_kernel(tc, x_words, x_scales, w1, w2, bg, w3, off
             for t in pair:
                 density(t)
             for t in pair:
-                fetch(e2, p2_t, t)
+                transmittance(e2, p2_t, t)
         for t in range(PACK):
-            fetch(e1, p1_t, t)
-        for u in range(2):
-            nc.scalar.copy(*weave(w3_bf[u][:], w3_raw[:, :, 256 * u : 256 * (u + 1)]))
+            transmittance(e1, p1_t, t)
+        for g, cols in enumerate(halves(N)):
+            nc.scalar.copy(*weave(w3_bf[g][:], w3_raw[:, :, cols]))
 
         for pair in pairs:
             for step in (far_share, far_blend, near_contrast):
@@ -180,26 +184,30 @@ def tile_picked_nerfvol_none_p_kernel(tc, x_words, x_scales, w1, w2, bg, w3, off
             near_share(t)
         quantise(w3_codes[0], w3_sc[0], w3_bf[0])
 
-        HV = V // 2
-        z_bf = tiles("z_bf", [P, HV * PACK], BF16, 2)
-        z_codes = tiles("z_codes", [P, HV], U32, 2)
-        z_sc = tiles("z_sc", [P, HV], U8, 2)
-        halves = [slice(0, HV), slice(HV, V)]
-        for h in range(2):
-            dst, src0 = weave(z_bf[h][:], behind[:, :, halves[h]])
-            dst, src1 = weave(z_bf[h][:], u1[:, :, halves[h]])
-            nc.vector.tensor_tensor(dst, src0, src1, ALU.subtract)
+        z_bf = tiles("z_bf", [P, V // 2 * PACK], BF16, 2)
+        z_codes = tiles("z_codes", [P, V // 2], U32, 2)
+        z_sc = tiles("z_sc", [P, V // 2], U8, 2)
+        for h, rays in enumerate(halves(V)):
+            z_view, behind_view = weave(z_bf[h][:], behind[:, :, rays])
+            z_view, u1_view = weave(z_bf[h][:], u1[:, :, rays])
+            nc.vector.tensor_tensor(z_view, behind_view, u1_view, ALU.subtract)
         quantise(z_codes[0], z_sc[0], z_bf[0])
         quantise(w3_codes[1], w3_sc[1], w3_bf[1])
         quantise(z_codes[1], z_sc[1], z_bf[1])
         out_rows = out.rearrange("(u p) v -> p u v", p=P)
-        for h in range(2):
-            for g in range(2):
-                acc = ps.tile([P, 2, HV], F32, name="val_ps%d" % (2 * h + g))
-                res = tile("res%d%d" % (h, g), [P, 2, HV], F32)
-                for u in range(2):
-                    cs = slice(P * u, P * (u + 1))
-                    nc.tensor.matmul_mx(out=acc[:, u, :], lhsT=w3_codes[g][:, cs].bitcast(FP8X4), lhsT_scale=w3_sc[g][:, cs],
-                                        rhs=z_codes[h][:].bitcast(FP8X4), rhs_scale=z_sc[h][:], start=True, stop=True)
-                cast(g == 0, res[:], acc[:])
-                nc.sync.dma_start(out_rows[:, 2 * g : 2 * g + 2, halves[h]], res[:])
+        for h, rays in enumerate(halves(V)):
+            for g, empty in enumerate((nc.scalar.copy, nc.vector.tensor_copy)):
+                acc = ps.tile([P, 2, V // 2], F32, name="val_ps%d" % (2 * h + g))
+                res = tile("res%d%d" % (h, g), [P, 2, V // 2], F32)
+                for n, cols in enumerate(halves(N // 2)):
+                    nc.tensor.matmul_mx(
+                        out=acc[:, n, :],
+                        lhsT=w3_codes[g][:, cols].bitcast(FP8X4),
+                        lhsT_scale=w3_sc[g][:, cols],
+                        rhs=z_codes[h][:].bitcast(FP8X4),
+                        rhs_scale=z_sc[h][:],
+                        start=True,
+                        stop=True,
+                    )
+                empty(res[:], acc[:])
+                nc.sync.dma_start(out_rows[:, 2 * g : 2 * g + 2, rays], res[:])

@@ -15,6 +15,7 @@ RUN = 4
 GROUP = 16
 QUADRANT = 32
 SCALE_ROWS = 4
+W1_AT = 4096
 FLOPS = 2 * (2 * K * H * S + H * N * V)
 
 
@@ -49,23 +50,27 @@ def tile_picked_nerfvol_none_p_kernel(tc, x_words, x_scales, w1, w2, bg, w3, off
         scales = shared.tile([P, T], U8, name="scales", offset=0, align_bytes=64)
         w2_raw = tile("w2_raw", [P, PACK, H], F32)
         zero_in = tile("zero_in", [P, 1], F32, "words")
-        zero_bias = tile("zero_bias", [P, 1], F32, "w1_raw")
+        zero_bias = shared.tile([P, PACK * H], F32, name="zero_bias", offset=W1_AT, align_bytes=64)
         one = tile("one", [P, 1], F32)
 
         nc.vector.memset(scales[:].bitcast(I32), 0)
         nc.vector.memset(zero_in[:], 0.0)
-        nc.vector.memset(zero_bias[:], 0.0)
+        nc.vector.memset(zero_bias[:, 0:1], 0.0)
         nc.sync.dma_start(offs_t[:], offs)
         nc.sync.dma_start(w2_raw[:], w2.rearrange("(p j) c -> p j c", j=PACK))
         nc.sync.dma_start(p2_t[:], p2)
         nc.sync.dma_start(p1_t[:], p1)
         for r in range(SCALE_ROWS):
             nc.sync.dma_start(scales[r:P:QUADRANT, :].bitcast(I32), x_scales[0, r : K // QUADRANT : SCALE_ROWS, :].bitcast(I32))
-        nc.scalar.activation(one[:], zero_in[:], ACT.Exp, bias=zero_bias[:])
+        nc.scalar.activation(one[:], zero_in[:], ACT.Exp, bias=zero_bias[:, 0:1])
         words = tile("words", [P, T], U32)
-        w1_raw = tile("w1_raw", [P, PACK, H], F32)
+        w1_raw = [
+            shared.tile([P, PACK, H // 2], F32, name="w1_raw%d" % c, offset=W1_AT + c * PACK * H * 2, align_bytes=64)
+            for c in range(2)
+        ]
         nc.sync.dma_start(words[:].bitcast(I32), x_words[0].rearrange("p n j -> p (n j)").bitcast(I32))
-        nc.sync.dma_start(w1_raw[:], w1.rearrange("(p j) c -> p j c", j=PACK))
+        for c, cols in enumerate(halves(H)):
+            nc.sync.dma_start(w1_raw[c][:], w1.rearrange("(p j) c -> p j c", j=PACK)[:, :, cols])
 
         x_codes = shared.tile([P, S], U32, name="x_codes", offset=PACK * P, align_bytes=64)
         x_bytes = tile("x_bytes", [P, S], U8)
@@ -106,9 +111,9 @@ def tile_picked_nerfvol_none_p_kernel(tc, x_words, x_scales, w1, w2, bg, w3, off
         for t in range(PACK):
             nc.sync.dma_start(w3_raw[:, t, :], w3_rows[t])
 
-        w1_bf = tile("w1_bf", [P, H * PACK], BF16)
-        w1_codes = tile("w1_codes", [P, H], U32)
-        w1_sc = tile("w1_sc", [P, H], U8)
+        w1_bf = [tiles("w1_bf%d" % c, [P, H], BF16, 2) for c in range(2)]
+        w1_codes = tiles("w1_codes", [P, P], U32)
+        w1_sc = tiles("w1_sc", [P, P], U8)
         val = tiles("val", [P, S], F32)
         dens = tiles("dens", [P, S], F32)
         e1 = tiles("e1_", [P, V], F32)
@@ -122,15 +127,14 @@ def tile_picked_nerfvol_none_p_kernel(tc, x_words, x_scales, w1, w2, bg, w3, off
         w3_codes = tiles("w3_codes", [P, N // 2], U32, 2)
         w3_sc = tiles("w3_sc", [P, N // 2], U8, 2)
 
-        def w1_round(t0, t1):
-            dst = w1_bf[:].rearrange("p (t a r j) -> p a t j r", t=PACK, r=RUN, j=PACK)
-            src = w1_raw[:].rearrange("p j (a t r) -> p a t j r", t=PACK, r=RUN)
-            nc.vector.tensor_copy(dst[:, :, t0:t1], src[:, :, t0:t1])
+        def w1_round(copy, c, g):
+            dst = w1_bf[c][g][:].rearrange("p (t a r j) -> p a t j r", t=2, r=RUN, j=PACK)
+            src = w1_raw[c][:].rearrange("p j (a t r) -> p a t j r", t=PACK, r=RUN)
+            copy(dst, src[:, :, 2 * g : 2 * g + 2])
 
-        def w1_project(t0, t1):
-            quantise(w1_codes[:, P * t0 : P * t1], w1_sc[:, P * t0 : P * t1], w1_bf[:, P * PACK * t0 : P * PACK * t1])
-            for t in range(t0, t1):
-                project(s_ps[t], w1_codes[:, P * t : P * (t + 1)], w1_sc[:, P * t : P * (t + 1)], slice(0, S))
+        def w1_quantise(c, t):
+            cols = halves(P)[c]
+            quantise(w1_codes[t][:, cols], w1_sc[t][:, cols], w1_bf[c][t // 2][:, halves(H)[t % 2]])
 
         def density(t):
             nc.scalar.activation(dens[t][:], s_ps[t][:], ACT.Relu)
@@ -153,15 +157,20 @@ def tile_picked_nerfvol_none_p_kernel(tc, x_words, x_scales, w1, w2, bg, w3, off
         def near_share(t):
             nc.vector.scalar_tensor_tensor(u1[:, t, :], e1[t][:], one[:], d1[t][:], ALU.subtract, ALU.mult)
 
-        for t in range(PACK):
+        for t in range(PACK - 1):
             nc.scalar.copy(val[t][:], val_ps[t][:])
-        w1_round(0, 1)
-        w1_round(1, 2)
-        w1_project(0, 1)
-        w1_project(1, 2)
-        w1_round(2, 4)
+        nc.scalar.copy(val[3][:, : S // 2], val_ps[3][:, : S // 2])
+        for g in range(2):
+            w1_round(nc.vector.tensor_copy, 0, g)
+        for t in range(PACK):
+            w1_quantise(0, t)
+        for g in range(2):
+            w1_round(nc.vector.tensor_copy, 1, g)
+        for t in range(PACK):
+            w1_quantise(1, t)
+            project(s_ps[t], w1_codes[t], w1_sc[t], slice(0, S))
         far_contrast(0)
-        w1_project(2, 4)
+        nc.vector.tensor_copy(val[3][:, S // 2 :], val_ps[3][:, S // 2 :])
         for t in range(1, PACK):
             far_contrast(t)
 

@@ -50,7 +50,7 @@ def tile_picked_nerfvol_none_p_kernel(tc, x_words, x_scales, w1, w2, bg, w3, off
         scales = shared.tile([P, T], U8, name="scales", offset=0, align_bytes=64)
         w2_raw = tile("w2_raw", [P, PACK, H], F32)
         zero_in = tile("zero_in", [P, 1], F32, "words")
-        zero_bias = shared.tile([P, PACK * H], F32, name="zero_bias", offset=W1_AT, align_bytes=64)
+        zero_bias = shared.tile([P, 2 * PACK * H], F32, name="zero_bias", offset=W1_AT, align_bytes=64)
         one = tile("one", [P, 1], F32)
 
         nc.vector.memset(scales[:].bitcast(I32), 0)
@@ -65,12 +65,12 @@ def tile_picked_nerfvol_none_p_kernel(tc, x_words, x_scales, w1, w2, bg, w3, off
         nc.scalar.activation(one[:], zero_in[:], ACT.Exp, bias=zero_bias[:, 0:1])
         words = tile("words", [P, T], U32)
         w1_raw = [
-            shared.tile([P, PACK, H // 2], F32, name="w1_raw%d" % c, offset=W1_AT + c * PACK * H * 2, align_bytes=64)
+            shared.tile([P, 2 * PACK, H // 2], F32, name="w1_raw%d" % c, offset=W1_AT + c * PACK * H * 4, align_bytes=64)
             for c in range(2)
         ]
         nc.sync.dma_start(words[:].bitcast(I32), x_words[0].rearrange("p n j -> p (n j)").bitcast(I32))
         for c, cols in enumerate(halves(H)):
-            nc.sync.dma_start(w1_raw[c][:], w1.rearrange("(p j) c -> p j c", j=PACK)[:, :, cols])
+            nc.sync.dma_start(w1_raw[c][:, :PACK], w1.rearrange("(p j) c -> p j c", j=PACK)[:, :, cols])
 
         x_codes = shared.tile([P, S], U32, name="x_codes", offset=PACK * P, align_bytes=64)
         x_bytes = tile("x_bytes", [P, S], U8)
@@ -111,10 +111,11 @@ def tile_picked_nerfvol_none_p_kernel(tc, x_words, x_scales, w1, w2, bg, w3, off
         for t in range(PACK):
             nc.sync.dma_start(w3_raw[:, t, :], w3_rows[t])
 
-        w1_bf = [tiles("w1_bf%d" % c, [P, H], BF16, 2) for c in range(2)]
+        groups = (((0, 1), (1, 4)), ((0, 2), (2, 4)))
+        w1_bf = [[tile("w1_bf%d%d" % (c, t0), [P, (t1 - t0) * H // 2], BF16) for t0, t1 in groups[c]] for c in range(2)]
         w1_codes = tiles("w1_codes", [P, P], U32)
         w1_sc = tiles("w1_sc", [P, P], U8)
-        val = tiles("val", [P, S], F32)
+        val = [shared.tile([P, S], F32, name="val%d" % t, offset=W1_AT + (t + t // 3) * S * 4, align_bytes=64) for t in range(PACK)]
         dens = tiles("dens", [P, S], F32)
         e1 = tiles("e1_", [P, V], F32)
         e2 = tiles("e2_", [P, V], F32)
@@ -128,13 +129,16 @@ def tile_picked_nerfvol_none_p_kernel(tc, x_words, x_scales, w1, w2, bg, w3, off
         w3_sc = tiles("w3_sc", [P, N // 2], U8, 2)
 
         def w1_round(copy, c, g):
-            dst = w1_bf[c][g][:].rearrange("p (t a r j) -> p a t j r", t=2, r=RUN, j=PACK)
-            src = w1_raw[c][:].rearrange("p j (a t r) -> p a t j r", t=PACK, r=RUN)
-            copy(dst, src[:, :, 2 * g : 2 * g + 2])
+            t0, t1 = groups[c][g]
+            dst = w1_bf[c][g][:].rearrange("p (t a r j) -> p a t j r", t=t1 - t0, r=RUN, j=PACK)
+            src = w1_raw[c][:, :PACK].rearrange("p j (a t r) -> p a t j r", t=PACK, r=RUN)
+            copy(dst, src[:, :, t0:t1])
 
         def w1_quantise(c, t):
             cols = halves(P)[c]
-            quantise(w1_codes[t][:, cols], w1_sc[t][:, cols], w1_bf[c][t // 2][:, halves(H)[t % 2]])
+            g = int(t >= groups[c][1][0])
+            first = (t - groups[c][g][0]) * H // 2
+            quantise(w1_codes[t][:, cols], w1_sc[t][:, cols], w1_bf[c][g][:, first : first + H // 2])
 
         def density(t):
             nc.scalar.activation(dens[t][:], s_ps[t][:], ACT.Relu)
@@ -157,11 +161,8 @@ def tile_picked_nerfvol_none_p_kernel(tc, x_words, x_scales, w1, w2, bg, w3, off
         def near_share(t):
             nc.vector.scalar_tensor_tensor(u1[:, t, :], e1[t][:], one[:], d1[t][:], ALU.subtract, ALU.mult)
 
-        for t in range(PACK - 1):
-            nc.scalar.copy(val[t][:], val_ps[t][:])
-        nc.scalar.copy(val[3][:, : S // 2], val_ps[3][:, : S // 2])
-        for g in range(2):
-            w1_round(nc.vector.tensor_copy, 0, g)
+        w1_round(nc.scalar.copy, 0, 1)
+        w1_round(nc.vector.tensor_copy, 0, 0)
         for t in range(PACK):
             w1_quantise(0, t)
         for g in range(2):
@@ -169,8 +170,10 @@ def tile_picked_nerfvol_none_p_kernel(tc, x_words, x_scales, w1, w2, bg, w3, off
         for t in range(PACK):
             w1_quantise(1, t)
             project(s_ps[t], w1_codes[t], w1_sc[t], slice(0, S))
+        for t in range(PACK - 1):
+            nc.scalar.copy(val[t][:], val_ps[t][:])
         far_contrast(0)
-        nc.vector.tensor_copy(val[3][:, S // 2 :], val_ps[3][:, S // 2 :])
+        nc.vector.tensor_copy(val[3][:], val_ps[3][:])
         for t in range(1, PACK):
             far_contrast(t)
 

@@ -88,13 +88,15 @@ def tile_picked_nerfvol_none_p_kernel(tc, x_words, x_scales, w1, w2, bg, w3, off
                 stop=True,
             )
 
-        nc.vector.tensor_copy(x_bytes[:], scales[:].indirect(offs_t[:]))
         w2_bf = tiles("w2_bf", [P, P * PACK], BF16)
         w2_codes = tiles("w2_codes", [P, P], U32)
         w2_sc = [shared.tile([P, P], U8, name="w2_sc%d" % t, offset=P * t, align_bytes=64) for t in range(PACK)]
         w2_cols = w2_raw[:].rearrange("p j (a t r) -> p t a j r", t=PACK, r=RUN)
         for t in range(PACK):
-            nc.scalar.copy(w2_bf[t][:].rearrange("p (a r j) -> p a j r", r=RUN, j=PACK), w2_cols[:, t])
+            copy = nc.vector.tensor_copy if t == 0 else nc.scalar.copy
+            copy(w2_bf[t][:].rearrange("p (a r j) -> p a j r", r=RUN, j=PACK), w2_cols[:, t])
+        nc.vector.tensor_copy(x_bytes[:], scales[:].indirect(offs_t[:]))
+        for t in range(PACK):
             quantise(w2_codes[t], w2_sc[t], w2_bf[t])
         for samples, entries in zip(halves(S), halves(S // GROUP)):
             nc.vector.tensor_copy(x_codes[:, samples], words[:].indirect(offs_t[:, entries]))
@@ -111,7 +113,7 @@ def tile_picked_nerfvol_none_p_kernel(tc, x_words, x_scales, w1, w2, bg, w3, off
         for t in range(PACK):
             nc.sync.dma_start(w3_raw[:, t, :], w3_rows[t])
 
-        groups = (((0, 1), (1, 4)), ((0, 2), (2, 4)))
+        groups = (((0, 2), (2, 4)), ((0, 2), (2, 4)))
         w1_bf = [[tile("w1_bf%d%d" % (c, t0), [P, (t1 - t0) * H // 2], BF16) for t0, t1 in groups[c]] for c in range(2)]
         w1_codes = tiles("w1_codes", [P, P], U32)
         w1_sc = tiles("w1_sc", [P, P], U8)
@@ -207,19 +209,30 @@ def tile_picked_nerfvol_none_p_kernel(tc, x_words, x_scales, w1, w2, bg, w3, off
         quantise(w3_codes[1], w3_sc[1], w3_bf[1])
         quantise(z_codes[1], z_sc[1], z_bf[1])
         out_rows = out.rearrange("(u p) v -> p u v", p=P)
+
+        def product(dst, u, h):
+            cols = halves(N // 2)[u % 2]
+            nc.tensor.matmul_mx(
+                out=dst,
+                lhsT=w3_codes[u // 2][:, cols].bitcast(FP8X4),
+                lhsT_scale=w3_sc[u // 2][:, cols],
+                rhs=z_codes[h][:].bitcast(FP8X4),
+                rhs_scale=z_sc[h][:],
+                start=True,
+                stop=True,
+            )
+
         for h, rays in enumerate(halves(V)):
             for g, empty in enumerate((nc.scalar.copy, nc.vector.tensor_copy)):
-                acc = ps.tile([P, 2, V // 2], F32, name="val_ps%d" % (2 * h + g))
                 res = tile("res%d%d" % (h, g), [P, 2, V // 2], F32)
-                for n, cols in enumerate(halves(N // 2)):
-                    nc.tensor.matmul_mx(
-                        out=acc[:, n, :],
-                        lhsT=w3_codes[g][:, cols].bitcast(FP8X4),
-                        lhsT_scale=w3_sc[g][:, cols],
-                        rhs=z_codes[h][:].bitcast(FP8X4),
-                        rhs_scale=z_sc[h][:],
-                        start=True,
-                        stop=True,
-                    )
-                empty(res[:], acc[:])
+                if (h, g) == (1, 1):
+                    for n in range(2):
+                        acc = ps.tile([P, V // 2], F32, name="s_ps%d" % n)
+                        product(acc[:], 2 * g + n, h)
+                        empty(res[:, n, :], acc[:])
+                else:
+                    acc = ps.tile([P, 2, V // 2], F32, name="val_ps%d" % (2 * h + g))
+                    for n in range(2):
+                        product(acc[:, n, :], 2 * g + n, h)
+                    empty(res[:], acc[:])
                 nc.sync.dma_start(out_rows[:, 2 * g : 2 * g + 2, rays], res[:])

@@ -15,7 +15,7 @@ RUN = 4
 GROUP = 16
 QUADRANT = 32
 SCALE_ROWS = 4
-W1_AT = 4096
+W2_AT, U2_AT, VAL_AT = 0, 20, 24
 FLOPS = 2 * (2 * K * H * S + H * N * V)
 
 
@@ -47,37 +47,40 @@ def tile_picked_nerfvol_none_p_kernel(tc, x_words, x_scales, w1, w2, bg, w3, off
         p1_t = lists.tile([P, V // GROUP], U16, name="p1_t")
         p2_t = lists.tile([P, V // GROUP], U16, name="p2_t")
 
-        scales = shared.tile([P, T], U8, name="scales", offset=0, align_bytes=64)
-        w2_raw = tile("w2_raw", [P, PACK, H], F32)
-        zero_in = tile("zero_in", [P, 1], F32, "words")
-        zero_bias = shared.tile([P, 2 * PACK * H], F32, name="zero_bias", offset=W1_AT, align_bytes=64)
+        def placed(name, shape, dtype, kib):
+            return shared.tile(shape, dtype, name=name, offset=kib * 1024, align_bytes=64)
+
+        words = tile("words", [P, T], U32)
+        scales = tile("scales", [P, T], U8)
+        seed = placed("seed", [P, 2 * PACK * H], F32, W2_AT)
+        zero = tile("zero", [P, 1], F32)
         one = tile("one", [P, 1], F32)
 
         nc.vector.memset(scales[:].bitcast(I32), 0)
-        nc.vector.memset(zero_in[:], 0.0)
-        nc.vector.memset(zero_bias[:, 0:1], 0.0)
+        nc.vector.memset(seed[:, 0:1], 0.0)
+        nc.vector.tensor_copy(zero[:], seed[:, 0:1])
         nc.sync.dma_start(offs_t[:], offs)
-        nc.sync.dma_start(w2_raw[:], w2.rearrange("(p j) c -> p j c", j=PACK))
+        nc.sync.dma_start(words[:].bitcast(I32), x_words[0].rearrange("p n j -> p (n j)").bitcast(I32))
         nc.sync.dma_start(p2_t[:], p2)
         nc.sync.dma_start(p1_t[:], p1)
         for r in range(SCALE_ROWS):
             nc.sync.dma_start(scales[r:P:QUADRANT, :].bitcast(I32), x_scales[0, r : K // QUADRANT : SCALE_ROWS, :].bitcast(I32))
-        nc.scalar.activation(one[:], zero_in[:], ACT.Exp, bias=zero_bias[:, 0:1])
-        words = tile("words", [P, T], U32)
-        w1_raw = [
-            shared.tile([P, 2 * PACK, H // 2], F32, name="w1_raw%d" % c, offset=W1_AT + c * PACK * H * 4, align_bytes=64)
-            for c in range(2)
-        ]
-        nc.sync.dma_start(words[:].bitcast(I32), x_words[0].rearrange("p n j -> p (n j)").bitcast(I32))
+        nc.scalar.activation(one[:], zero[:], ACT.Exp)
+        w2_raw = placed("w2_raw", [P, PACK, H], F32, W2_AT)
+        w1_raw = [placed("w1_raw%d" % c, [P, PACK, H // 2], F32, at) for c, at in enumerate((W2_AT + 8, W2_AT + 12))]
+        w1_cols = w1.rearrange("(p j) c -> p j c", j=PACK)
+        nc.sync.dma_start(w2_raw[:], w2.rearrange("(p j) c -> p j c", j=PACK))
         for c, cols in enumerate(halves(H)):
-            nc.sync.dma_start(w1_raw[c][:, :PACK], w1.rearrange("(p j) c -> p j c", j=PACK)[:, :, cols])
+            nc.sync.dma_start(w1_raw[c][:], w1_cols[:, :, cols])
 
-        x_codes = shared.tile([P, S], U32, name="x_codes", offset=PACK * P, align_bytes=64)
         x_bytes = tile("x_bytes", [P, S], U8)
-        s_ps = [ps.tile([P, S], F32, name="s_ps%d" % t) for t in range(PACK)]
+        x_codes = tile("x_codes", [P, S], U32)
+        nc.vector.tensor_copy(x_codes[:], words[:].indirect(offs_t[:]))
+        nc.vector.tensor_copy(x_bytes[:], scales[:].indirect(offs_t[:]))
+        s_ps = [ps.tile([P, S], F32, name="s_ps%d" % t) for t in range(PACK - 1)]
         val_ps = [ps.tile([P, S], F32, name="val_ps%d" % t) for t in range(PACK)]
 
-        def project(bank, codes, scale_bytes, samples):
+        def project(bank, codes, scale_bytes, samples=slice(0, S)):
             nc.tensor.matmul_mx(
                 out=bank[:, samples],
                 lhsT=codes[:].bitcast(FP8X4),
@@ -88,62 +91,70 @@ def tile_picked_nerfvol_none_p_kernel(tc, x_words, x_scales, w1, w2, bg, w3, off
                 stop=True,
             )
 
-        w2_bf = tiles("w2_bf", [P, P * PACK], BF16)
-        w2_codes = tiles("w2_codes", [P, P], U32)
-        w2_sc = [shared.tile([P, P], U8, name="w2_sc%d" % t, offset=P * t, align_bytes=64) for t in range(PACK)]
-        w2_cols = w2_raw[:].rearrange("p j (a t r) -> p t a j r", t=PACK, r=RUN)
-        for t in range(PACK):
-            copy = nc.vector.tensor_copy if t == 0 else nc.scalar.copy
-            copy(w2_bf[t][:].rearrange("p (a r j) -> p a j r", r=RUN, j=PACK), w2_cols[:, t])
-        nc.vector.tensor_copy(x_bytes[:], scales[:].indirect(offs_t[:]))
-        for t in range(PACK):
-            quantise(w2_codes[t], w2_sc[t], w2_bf[t])
-        for samples, entries in zip(halves(S), halves(S // GROUP)):
-            nc.vector.tensor_copy(x_codes[:, samples], words[:].indirect(offs_t[:, entries]))
-        for t in range(PACK):
-            for samples in halves(S):
-                project(val_ps[t], w2_codes[t], w2_sc[t], samples)
+        def round_tiles(copy, dst, raw, t0, t1):
+            dst = dst.rearrange("p (t a r j) -> p a t j r", t=t1 - t0, r=RUN, j=PACK)
+            src = raw[:].rearrange("p j (a t r) -> p a t j r", t=PACK, r=RUN)
+            copy(dst, src[:, :, t0:t1])
 
         bg_rows = bg.rearrange("(a t r) v -> t a r v", t=PACK, r=RUN)
         w3_rows = w3.rearrange("(a t r) m -> t a r m", t=PACK, r=RUN)
-        bg_all = tile("bg_all", [P, PACK, V], F32, "w2_raw")
+        bg_all = tile("bg_all", [P, PACK, V], F32, "words")
         for t in range(PACK):
             nc.sync.dma_start(bg_all[:, t, :], bg_rows[t])
-        w3_raw = tile("w3_raw", [P, PACK, N], F32, "words")
+
+        w2_bf = tiles("w2_bf", [P, H], BF16)
+        w2_codes = tiles("w2_codes", [P, P], U32)
+        w2_sc = tiles("w2_sc", [P, P], U8)
+        for t in range(PACK):
+            round_tiles(nc.vector.tensor_copy if t < 2 else nc.scalar.copy, w2_bf[t][:], w2_raw, t, t + 1)
+        for t in range(PACK):
+            quantise(w2_codes[t], w2_sc[t], w2_bf[t])
+            project(val_ps[t], w2_codes[t], w2_sc[t])
+        w3_raw = placed("w3_raw", [P, PACK, N], F32, W2_AT)
         for t in range(PACK):
             nc.sync.dma_start(w3_raw[:, t, :], w3_rows[t])
 
-        groups = (((0, 2), (2, 4)), ((0, 2), (2, 4)))
-        w1_bf = [[tile("w1_bf%d%d" % (c, t0), [P, (t1 - t0) * H // 2], BF16) for t0, t1 in groups[c]] for c in range(2)]
+        HALF = H // 2
         w1_codes = tiles("w1_codes", [P, P], U32)
         w1_sc = tiles("w1_sc", [P, P], U8)
-        val = [shared.tile([P, S], F32, name="val%d" % t, offset=W1_AT + (t + t // 3) * S * 4, align_bytes=64) for t in range(PACK)]
+        w1_bf = tiles("w1_bf", [P, H], BF16, 2) + [tile("w1_bf2", [P, 2 * H], BF16)]
+
+        def w1_round(n, c, t0, t1):
+            dst = w1_bf[n][:].rearrange("p (t c a r j) -> p c a t j r", t=t1 - t0, c=2, r=RUN, j=PACK)[:, c]
+            src = w1_raw[c][:].rearrange("p j (a t r) -> p a t j r", t=PACK, r=RUN)
+            nc.vector.tensor_copy(dst, src[:, :, t0:t1])
+
+        for n, (t0, t1) in enumerate(((0, 1), (1, 2), (2, 4))):
+            w1_round(n, 0, t0, t1)
+        w1_round(0, 1, 0, 1)
+        w1_round(1, 1, 1, 2)
+        quantise(w1_codes[0], w1_sc[0], w1_bf[0])
+        w1_round(2, 1, 2, 4)
+        quantise(w1_codes[1], w1_sc[1], w1_bf[1])
+        for t in (2, 3):
+            quantise(w1_codes[t], w1_sc[t], w1_bf[2][:, (t - 2) * H : (t - 1) * H])
+        first, second = halves(S)
+        s1_second = ps.tile([P, S], F32, name="s_ps3")
+        project(s_ps[0], w1_codes[0], w1_sc[0])
+        project(s_ps[1], w1_codes[1], w1_sc[1], first)
+        project(s1_second, w1_codes[1], w1_sc[1], second)
+        project(s_ps[2], w1_codes[2], w1_sc[2])
+
+        val = [placed("val%d" % t, [P, S], F32, VAL_AT + 2 * t) for t in range(PACK)]
         dens = tiles("dens", [P, S], F32)
-        e1 = tiles("e1_", [P, V], F32)
         e2 = tiles("e2_", [P, V], F32)
-        d1 = tiles("d1_", [P, V], F32)
+        d1_all = tile("d1", [P, PACK, V], F32)
+        d1 = [d1_all[:, t, :] for t in range(PACK)]
         d2 = tiles("d2_", [P, V], F32)
-        u2 = tiles("u2_", [P, V], F32)
-        u1 = tile("u1", [P, PACK, V], F32)
+        u2 = [placed("u2_%d" % t, [P, V], F32, U2_AT + t) for t in range(PACK)]
         behind = tile("behind", [P, PACK, V], F32)
         w3_bf = [tile("w3_bf%d" % g, [P, N * PACK // 2], BF16, "dens%d" % g) for g in range(2)]
-        w3_codes = tiles("w3_codes", [P, N // 2], U32, 2)
+        w3_codes = [None, tile("w3_codes1", [P, N // 2], U32)]
         w3_sc = tiles("w3_sc", [P, N // 2], U8, 2)
 
-        def w1_round(copy, c, g):
-            t0, t1 = groups[c][g]
-            dst = w1_bf[c][g][:].rearrange("p (t a r j) -> p a t j r", t=t1 - t0, r=RUN, j=PACK)
-            src = w1_raw[c][:, :PACK].rearrange("p j (a t r) -> p a t j r", t=PACK, r=RUN)
-            copy(dst, src[:, :, t0:t1])
-
-        def w1_quantise(c, t):
-            cols = halves(P)[c]
-            g = int(t >= groups[c][1][0])
-            first = (t - groups[c][g][0]) * H // 2
-            quantise(w1_codes[t][:, cols], w1_sc[t][:, cols], w1_bf[c][g][:, first : first + H // 2])
-
         def density(t):
-            nc.scalar.activation(dens[t][:], s_ps[t][:], ACT.Relu)
+            samples = first if t == 1 else slice(0, S)
+            nc.scalar.activation(dens[t][:, samples], s_ps[t][:, samples], ACT.Relu)
 
         def transmittance(e, list_t, t):
             nc.scalar.activation(e[t][:], dens[t][:].indirect(list_t[:]), ACT.Exp, scale=-1.0)
@@ -160,52 +171,59 @@ def tile_picked_nerfvol_none_p_kernel(tc, x_words, x_scales, w1, w2, bg, w3, off
         def near_contrast(t):
             nc.vector.tensor_tensor(d1[t][:], val[t][:].indirect(p1_t[:]), behind[:, t, :], ALU.subtract)
 
-        def near_share(t):
-            nc.vector.scalar_tensor_tensor(u1[:, t, :], e1[t][:], one[:], d1[t][:], ALU.subtract, ALU.mult)
+        def near_share(ts, rays):
+            nc.vector.scalar_tensor_tensor(u1[:, ts, rays], e1_all[:, ts, rays], one[:], d1_all[:, ts, rays], ALU.subtract, ALU.mult)
 
-        w1_round(nc.scalar.copy, 0, 1)
-        w1_round(nc.vector.tensor_copy, 0, 0)
         for t in range(PACK):
-            w1_quantise(0, t)
-        for g in range(2):
-            w1_round(nc.vector.tensor_copy, 1, g)
-        for t in range(PACK):
-            w1_quantise(1, t)
-            project(s_ps[t], w1_codes[t], w1_sc[t], slice(0, S))
-        for t in range(PACK - 1):
             nc.scalar.copy(val[t][:], val_ps[t][:])
+        s_ps.append(ps.tile([P, S], F32, name="val_ps0"))
+        project(s_ps[3], w1_codes[3], w1_sc[3])
         far_contrast(0)
-        nc.vector.tensor_copy(val[3][:], val_ps[3][:])
+        nc.vector.tensor_scalar_max(dens[1][:, second], s1_second[:, second], 0.0)
         for t in range(1, PACK):
             far_contrast(t)
 
-        pairs = ((0, 1), (2, 3))
-        for pair in pairs:
+        def far_lookups(pair):
             for t in pair:
                 density(t)
             for t in pair:
                 transmittance(e2, p2_t, t)
+
+        def far_steps(pair):
+            for step in (far_share, far_blend, near_contrast):
+                for t in pair:
+                    step(t)
+
+        far_lookups((0, 1))
+        far_steps((0, 1))
+        far_lookups((2, 3))
+        e1_all = placed("e1", [P, PACK, V], F32, U2_AT - 2)
+        e1 = [e1_all[:, t, :] for t in range(PACK)]
         for t in range(PACK):
             transmittance(e1, p1_t, t)
         for g, cols in enumerate(halves(N)):
             nc.scalar.copy(*weave(w3_bf[g][:], w3_raw[:, :, cols]))
+        far_steps((2, 3))
+        u1 = placed("u1", [P, PACK, V], F32, VAL_AT + 2)
+        near_share(slice(0, 2), slice(0, V))
+        for rays in halves(V):
+            near_share(slice(2, 4), rays)
 
-        for pair in pairs:
-            for step in (far_share, far_blend, near_contrast):
-                for t in pair:
-                    step(t)
-        for t in range(PACK):
-            near_share(t)
-        quantise(w3_codes[0], w3_sc[0], w3_bf[0])
-
-        z_bf = tiles("z_bf", [P, V // 2 * PACK], BF16, 2)
+        z_bf = [tile("z_bf0", [P, V // 2 * PACK], BF16), tile("z_bf1", [P, V // 2 * PACK], BF16, "dens0")]
         z_codes = tiles("z_codes", [P, V // 2], U32, 2)
         z_sc = tiles("z_sc", [P, V // 2], U8, 2)
-        for h, rays in enumerate(halves(V)):
+
+        def blend(h):
+            rays = halves(V)[h]
             z_view, behind_view = weave(z_bf[h][:], behind[:, :, rays])
             z_view, u1_view = weave(z_bf[h][:], u1[:, :, rays])
             nc.vector.tensor_tensor(z_view, behind_view, u1_view, ALU.subtract)
+
+        w3_codes[0] = placed("w3_codes0", [P, N // 2], U32, U2_AT - 2)
+        blend(0)
+        quantise(w3_codes[0], w3_sc[0], w3_bf[0])
         quantise(z_codes[0], z_sc[0], z_bf[0])
+        blend(1)
         quantise(w3_codes[1], w3_sc[1], w3_bf[1])
         quantise(z_codes[1], z_sc[1], z_bf[1])
         out_rows = out.rearrange("(u p) v -> p u v", p=P)

@@ -77,16 +77,16 @@ def tile_picked_nerfvol_none_p_kernel(tc, x_words, x_scales, w1, w2, bg, w3, off
         x_codes = tile("x_codes", [P, S], U32)
         nc.vector.tensor_copy(x_codes[:], words[:].indirect(offs_t[:]))
         nc.vector.tensor_copy(x_bytes[:], scales[:].indirect(offs_t[:]))
-        s_ps = [ps.tile([P, S], F32, name="s_ps%d" % t) for t in range(PACK - 1)]
+        s_ps = [ps.tile([P, S], F32, name="s_ps%d" % t) for t in range(PACK)]
         val_ps = [ps.tile([P, S], F32, name="val_ps%d" % t) for t in range(PACK)]
 
-        def project(bank, codes, scale_bytes, samples=slice(0, S)):
+        def project(bank, codes, scale_bytes):
             nc.tensor.matmul_mx(
-                out=bank[:, samples],
+                out=bank[:],
                 lhsT=codes[:].bitcast(FP8X4),
                 lhsT_scale=scale_bytes[:],
-                rhs=x_codes[:, samples].bitcast(FP8X4),
-                rhs_scale=x_bytes[:, samples],
+                rhs=x_codes[:].bitcast(FP8X4),
+                rhs_scale=x_bytes[:],
                 start=True,
                 stop=True,
             )
@@ -106,7 +106,7 @@ def tile_picked_nerfvol_none_p_kernel(tc, x_words, x_scales, w1, w2, bg, w3, off
         w2_codes = tiles("w2_codes", [P, P], U32)
         w2_sc = tiles("w2_sc", [P, P], U8)
         for t in range(PACK):
-            round_tiles(nc.vector.tensor_copy if t < 2 else nc.scalar.copy, w2_bf[t][:], w2_raw, t, t + 1)
+            round_tiles(nc.vector.tensor_copy if t % 2 == 0 else nc.scalar.copy, w2_bf[t][:], w2_raw, t, t + 1)
         for t in range(PACK):
             quantise(w2_codes[t], w2_sc[t], w2_bf[t])
             project(val_ps[t], w2_codes[t], w2_sc[t])
@@ -117,28 +117,26 @@ def tile_picked_nerfvol_none_p_kernel(tc, x_words, x_scales, w1, w2, bg, w3, off
         HALF = H // 2
         w1_codes = tiles("w1_codes", [P, P], U32)
         w1_sc = tiles("w1_sc", [P, P], U8)
-        w1_bf = tiles("w1_bf", [P, H], BF16, 2) + [tile("w1_bf2", [P, 2 * H], BF16)]
+        groups = ((0, 1), (1, 3), (3, 4))
+        w1_bf = [tile("w1_bf%d" % t0, [P, (t1 - t0) * H], BF16) for t0, t1 in groups]
 
-        def w1_round(n, c, t0, t1):
+        def w1_round(n, c):
+            t0, t1 = groups[n]
             dst = w1_bf[n][:].rearrange("p (t c a r j) -> p c a t j r", t=t1 - t0, c=2, r=RUN, j=PACK)[:, c]
             src = w1_raw[c][:].rearrange("p j (a t r) -> p a t j r", t=PACK, r=RUN)
             nc.vector.tensor_copy(dst, src[:, :, t0:t1])
 
-        for n, (t0, t1) in enumerate(((0, 1), (1, 2), (2, 4))):
-            w1_round(n, 0, t0, t1)
-        w1_round(0, 1, 0, 1)
-        w1_round(1, 1, 1, 2)
+        for n in range(3):
+            w1_round(n, 0)
+        w1_round(0, 1)
+        w1_round(1, 1)
         quantise(w1_codes[0], w1_sc[0], w1_bf[0])
-        w1_round(2, 1, 2, 4)
-        quantise(w1_codes[1], w1_sc[1], w1_bf[1])
-        for t in (2, 3):
-            quantise(w1_codes[t], w1_sc[t], w1_bf[2][:, (t - 2) * H : (t - 1) * H])
-        first, second = halves(S)
-        s1_second = ps.tile([P, S], F32, name="s_ps3")
-        project(s_ps[0], w1_codes[0], w1_sc[0])
-        project(s_ps[1], w1_codes[1], w1_sc[1], first)
-        project(s1_second, w1_codes[1], w1_sc[1], second)
-        project(s_ps[2], w1_codes[2], w1_sc[2])
+        w1_round(2, 1)
+        for t in (1, 2):
+            quantise(w1_codes[t], w1_sc[t], w1_bf[1][:, (t - 1) * H : t * H])
+        quantise(w1_codes[3], w1_sc[3], w1_bf[2])
+        for t in range(PACK):
+            project(s_ps[t], w1_codes[t], w1_sc[t])
 
         val = [placed("val%d" % t, [P, S], F32, VAL_AT + 2 * t) for t in range(PACK)]
         dens = tiles("dens", [P, S], F32)
@@ -153,8 +151,7 @@ def tile_picked_nerfvol_none_p_kernel(tc, x_words, x_scales, w1, w2, bg, w3, off
         w3_sc = tiles("w3_sc", [P, N // 2], U8, 2)
 
         def density(t):
-            samples = first if t == 1 else slice(0, S)
-            nc.scalar.activation(dens[t][:, samples], s_ps[t][:, samples], ACT.Relu)
+            nc.scalar.activation(dens[t][:], s_ps[t][:], ACT.Relu)
 
         def transmittance(e, list_t, t):
             nc.scalar.activation(e[t][:], dens[t][:].indirect(list_t[:]), ACT.Exp, scale=-1.0)
@@ -176,11 +173,7 @@ def tile_picked_nerfvol_none_p_kernel(tc, x_words, x_scales, w1, w2, bg, w3, off
 
         for t in range(PACK):
             nc.scalar.copy(val[t][:], val_ps[t][:])
-        s_ps.append(ps.tile([P, S], F32, name="val_ps0"))
-        project(s_ps[3], w1_codes[3], w1_sc[3])
-        far_contrast(0)
-        nc.vector.tensor_scalar_max(dens[1][:, second], s1_second[:, second], 0.0)
-        for t in range(1, PACK):
+        for t in range(PACK):
             far_contrast(t)
 
         def far_lookups(pair):
@@ -205,11 +198,12 @@ def tile_picked_nerfvol_none_p_kernel(tc, x_words, x_scales, w1, w2, bg, w3, off
             nc.scalar.copy(*weave(w3_bf[g][:], w3_raw[:, :, cols]))
         far_steps((2, 3))
         u1 = placed("u1", [P, PACK, V], F32, VAL_AT + 2)
-        near_share(slice(0, 2), slice(0, V))
-        for rays in halves(V):
-            near_share(slice(2, 4), rays)
+        first, second = halves(V)
+        near_share(slice(0, 3), first)
+        near_share(slice(3, 4), first)
+        near_share(slice(0, 4), second)
 
-        z_bf = [tile("z_bf0", [P, V // 2 * PACK], BF16), tile("z_bf1", [P, V // 2 * PACK], BF16, "dens0")]
+        z_bf = [tile("z_bf0", [P, V // 2 * PACK], BF16), tile("z_bf1", [P, V // 2 * PACK], BF16)]
         z_codes = tiles("z_codes", [P, V // 2], U32, 2)
         z_sc = tiles("z_sc", [P, V // 2], U8, 2)
 
@@ -221,9 +215,9 @@ def tile_picked_nerfvol_none_p_kernel(tc, x_words, x_scales, w1, w2, bg, w3, off
 
         w3_codes[0] = placed("w3_codes0", [P, N // 2], U32, U2_AT - 2)
         blend(0)
+        blend(1)
         quantise(w3_codes[0], w3_sc[0], w3_bf[0])
         quantise(z_codes[0], z_sc[0], z_bf[0])
-        blend(1)
         quantise(w3_codes[1], w3_sc[1], w3_bf[1])
         quantise(z_codes[1], z_sc[1], z_bf[1])
         out_rows = out.rearrange("(u p) v -> p u v", p=P)

@@ -67,11 +67,11 @@ def tile_picked_nerfvol_none_p_kernel(tc, x_words, x_scales, w1, w2, bg, w3, off
             nc.sync.dma_start(scales[r:P:QUADRANT, :].bitcast(I32), x_scales[0, r : K // QUADRANT : SCALE_ROWS, :].bitcast(I32))
         nc.scalar.activation(one[:], zero[:], ACT.Exp)
         w2_raw = placed("w2_raw", [P, PACK, H], F32, W2_AT)
-        w1_raw = [placed("w1_raw%d" % c, [P, PACK, H // 2], F32, at) for c, at in enumerate((W2_AT + 8, W2_AT + 12))]
+        w1_raw = [placed("w1_raw%d" % c, [P, PACK // 2, H], F32, at) for c, at in enumerate((W2_AT + 8, W2_AT + 12))]
         w1_cols = w1.rearrange("(p j) c -> p j c", j=PACK)
         nc.sync.dma_start(w2_raw[:], w2.rearrange("(p j) c -> p j c", j=PACK))
-        for c, cols in enumerate(halves(H)):
-            nc.sync.dma_start(w1_raw[c][:], w1_cols[:, :, cols])
+        for c, rows in enumerate(halves(PACK)):
+            nc.sync.dma_start(w1_raw[c][:], w1_cols[:, rows])
 
         x_bytes = tile("x_bytes", [P, S], U8)
         x_codes = tile("x_codes", [P, S], U32)
@@ -114,7 +114,6 @@ def tile_picked_nerfvol_none_p_kernel(tc, x_words, x_scales, w1, w2, bg, w3, off
         for t in range(PACK):
             nc.sync.dma_start(w3_raw[:, t, :], w3_rows[t])
 
-        HALF = H // 2
         w1_codes = tiles("w1_codes", [P, P], U32)
         w1_sc = tiles("w1_sc", [P, P], U8)
         groups = ((0, 1), (1, 3), (3, 4))
@@ -122,7 +121,7 @@ def tile_picked_nerfvol_none_p_kernel(tc, x_words, x_scales, w1, w2, bg, w3, off
 
         def w1_round(n, c):
             t0, t1 = groups[n]
-            dst = w1_bf[n][:].rearrange("p (t c a r j) -> p c a t j r", t=t1 - t0, c=2, r=RUN, j=PACK)[:, c]
+            dst = w1_bf[n][:].rearrange("p (t a r j) -> p a t j r", t=t1 - t0, r=RUN, j=PACK)[:, :, :, halves(PACK)[c]]
             src = w1_raw[c][:].rearrange("p j (a t r) -> p a t j r", t=PACK, r=RUN)
             nc.vector.tensor_copy(dst, src[:, :, t0:t1])
 

@@ -15,6 +15,7 @@ RUN = 4
 GROUP = 16
 QUADRANT = 32
 SCALE_ROWS = 4
+SCALES_AT = P - K // QUADRANT
 W2_AT, U2_AT, VAL_AT = 0, 20, 24
 FLOPS = 2 * (2 * K * H * S + H * N * V)
 
@@ -51,32 +52,34 @@ def tile_picked_nerfvol_none_p_kernel(tc, x_words, x_scales, w1, w2, bg, w3, off
             return shared.tile(shape, dtype, name=name, offset=kib * 1024, align_bytes=64)
 
         words = tile("words", [P, T], U32)
-        scales = tile("scales", [P, T], U8)
-        seed = placed("seed", [P, 2 * PACK * H], F32, W2_AT)
+        scales = placed("scales", [P, T], U8, W2_AT + 11)
+        x_bytes = tile("x_bytes", [P, S], U8)
         zero = tile("zero", [P, 1], F32)
         one = tile("one", [P, 1], F32)
 
-        nc.vector.memset(scales[:].bitcast(I32), 0)
-        nc.vector.memset(seed[:, 0:1], 0.0)
-        nc.vector.tensor_copy(zero[:], seed[:, 0:1])
-        nc.sync.dma_start(offs_t[:], offs)
-        nc.sync.dma_start(words[:].bitcast(I32), x_words[0].rearrange("p n j -> p (n j)").bitcast(I32))
-        nc.sync.dma_start(p2_t[:], p2)
-        nc.sync.dma_start(p1_t[:], p1)
-        for r in range(SCALE_ROWS):
-            nc.sync.dma_start(scales[r:P:QUADRANT, :].bitcast(I32), x_scales[0, r : K // QUADRANT : SCALE_ROWS, :].bitcast(I32))
-        nc.scalar.activation(one[:], zero[:], ACT.Exp)
+        nc.vector.memset(zero[:], 0.0)
+        nc.vector.memset(scales[:SCALES_AT, :].bitcast(I32), 0)
+        nc.vector.memset(x_bytes[:].bitcast(I32), 0)
         w2_raw = placed("w2_raw", [P, PACK, H], F32, W2_AT)
+        nc.sync.dma_start(scales[SCALES_AT:, :].bitcast(I32), x_scales[0].bitcast(I32))
+        nc.sync.dma_start(offs_t[:], offs)
+        nc.sync.dma_start(p2_t[:], p2)
+        nc.sync.dma_start(words[:].bitcast(I32), x_words[0].rearrange("p n j -> p (n j)").bitcast(I32))
+        nc.sync.dma_start(w2_raw[:], w2.rearrange("(p j) c -> p j c", j=PACK))
+        nc.sync.dma_start(p1_t[:], p1)
+        nc.scalar.activation(one[:], zero[:], ACT.Exp)
+
+        picked_scales = tile("picked_scales", [P, S], U8)
+        x_codes = tile("x_codes", [P, S], U32)
+        nc.vector.tensor_copy(picked_scales[:], scales[:].indirect(offs_t[:]))
+        for q in range(P // QUADRANT):
+            rows = slice(SCALES_AT + SCALE_ROWS * q, SCALES_AT + SCALE_ROWS * (q + 1))
+            nc.sync.dma_start(x_bytes[QUADRANT * q : QUADRANT * q + SCALE_ROWS, :].bitcast(I32), picked_scales[rows, :].bitcast(I32))
         w1_raw = [placed("w1_raw%d" % c, [P, PACK // 2, H], F32, at) for c, at in enumerate((W2_AT + 8, W2_AT + 12))]
         w1_cols = w1.rearrange("(p j) c -> p j c", j=PACK)
-        nc.sync.dma_start(w2_raw[:], w2.rearrange("(p j) c -> p j c", j=PACK))
         for c, rows in enumerate(halves(PACK)):
             nc.sync.dma_start(w1_raw[c][:], w1_cols[:, rows])
-
-        x_bytes = tile("x_bytes", [P, S], U8)
-        x_codes = tile("x_codes", [P, S], U32)
         nc.vector.tensor_copy(x_codes[:], words[:].indirect(offs_t[:]))
-        nc.vector.tensor_copy(x_bytes[:], scales[:].indirect(offs_t[:]))
         s_ps = [ps.tile([P, S], F32, name="s_ps%d" % t) for t in range(PACK)]
         val_ps = [ps.tile([P, S], F32, name="val_ps%d" % t) for t in range(PACK)]
 

@@ -16,7 +16,7 @@ GROUP = 16
 QUADRANT = 32
 SCALE_ROWS = 4
 SCALES_AT = P - K // QUADRANT
-W2_AT, U2_AT, VAL_AT = 0, 20, 24
+W2_AT, BG_AT, U2_AT, VAL_AT = 0, 0, 20, 24
 FLOPS = 2 * (2 * K * H * S + H * N * V)
 
 
@@ -61,16 +61,17 @@ def tile_picked_nerfvol_none_p_kernel(tc, x_words, x_scales, w1, w2, bg, w3, off
         nc.vector.memset(scales[:SCALES_AT, :].bitcast(I32), 0)
         nc.vector.memset(x_bytes[:].bitcast(I32), 0)
         w2_raw = placed("w2_raw", [P, PACK, H], F32, W2_AT)
-        nc.sync.dma_start(scales[SCALES_AT:, :].bitcast(I32), x_scales[0].bitcast(I32))
         nc.sync.dma_start(offs_t[:], offs)
+        nc.scalar.dma_start(scales[SCALES_AT:, :].bitcast(I32), x_scales[0].bitcast(I32))
+        nc.sync.dma_start(w2_raw[:], w2.rearrange("(p j) c -> p j c", j=PACK))
         nc.sync.dma_start(p2_t[:], p2)
         nc.sync.dma_start(words[:].bitcast(I32), x_words[0].rearrange("p n j -> p (n j)").bitcast(I32))
-        nc.sync.dma_start(w2_raw[:], w2.rearrange("(p j) c -> p j c", j=PACK))
         nc.sync.dma_start(p1_t[:], p1)
         nc.scalar.activation(one[:], zero[:], ACT.Exp)
 
         picked_scales = tile("picked_scales", [P, S], U8)
-        x_codes = tile("x_codes", [P, S], U32)
+        x_codes = tiles("x_codes", [P, S // 2], U32, 2)
+        samples = halves(S)
         nc.vector.tensor_copy(picked_scales[:], scales[:].indirect(offs_t[:]))
         for q in range(P // QUADRANT):
             rows = slice(SCALES_AT + SCALE_ROWS * q, SCALES_AT + SCALE_ROWS * (q + 1))
@@ -79,17 +80,16 @@ def tile_picked_nerfvol_none_p_kernel(tc, x_words, x_scales, w1, w2, bg, w3, off
         w1_cols = w1.rearrange("(p j) c -> p j c", j=PACK)
         for c, rows in enumerate(halves(PACK)):
             nc.sync.dma_start(w1_raw[c][:], w1_cols[:, rows])
-        nc.vector.tensor_copy(x_codes[:], words[:].indirect(offs_t[:]))
-        s_ps = [ps.tile([P, S], F32, name="s_ps%d" % t) for t in range(PACK)]
         val_ps = [ps.tile([P, S], F32, name="val_ps%d" % t) for t in range(PACK)]
 
-        def project(bank, codes, scale_bytes):
+        def project(bank, codes, scale_bytes, h):
+            cols = samples[h]
             nc.tensor.matmul_mx(
-                out=bank[:],
+                out=bank,
                 lhsT=codes[:].bitcast(FP8X4),
                 lhsT_scale=scale_bytes[:],
-                rhs=x_codes[:].bitcast(FP8X4),
-                rhs_scale=x_bytes[:],
+                rhs=x_codes[h][:].bitcast(FP8X4),
+                rhs_scale=x_bytes[:, cols],
                 start=True,
                 stop=True,
             )
@@ -101,9 +101,6 @@ def tile_picked_nerfvol_none_p_kernel(tc, x_words, x_scales, w1, w2, bg, w3, off
 
         bg_rows = bg.rearrange("(a t r) v -> t a r v", t=PACK, r=RUN)
         w3_rows = w3.rearrange("(a t r) m -> t a r m", t=PACK, r=RUN)
-        bg_all = tile("bg_all", [P, PACK, V], F32, "words")
-        for t in range(PACK):
-            nc.sync.dma_start(bg_all[:, t, :], bg_rows[t])
 
         w2_bf = tiles("w2_bf", [P, H], BF16)
         w2_codes = tiles("w2_codes", [P, P], U32)
@@ -112,8 +109,24 @@ def tile_picked_nerfvol_none_p_kernel(tc, x_words, x_scales, w1, w2, bg, w3, off
             round_tiles(nc.vector.tensor_copy if t % 2 == 0 else nc.scalar.copy, w2_bf[t][:], w2_raw, t, t + 1)
         for t in range(PACK):
             quantise(w2_codes[t], w2_sc[t], w2_bf[t])
-            project(val_ps[t], w2_codes[t], w2_sc[t])
-        w3_raw = placed("w3_raw", [P, PACK, N], F32, W2_AT)
+        for h, cols in enumerate(samples):
+            nc.vector.tensor_copy(x_codes[h][:], words[:].indirect(offs_t[:, halves(S // GROUP)[h]]))
+        val = [placed("val%d" % t, [P, S], F32, VAL_AT + 2 * t) for t in range(PACK)]
+        early = [ps.tile([P, S // 2], F32, name="s_ps%d" % (2 + t)) for t in range(2)]
+        for t in range(2):
+            project(early[t][:], w2_codes[t], w2_sc[t], 0)
+            nc.scalar.copy(val[t][:, samples[0]], early[t][:])
+        for t in range(2):
+            project(val_ps[t][:, samples[1]], w2_codes[t], w2_sc[t], 1)
+        nc.scalar.copy(val[0][:, samples[1]], val_ps[0][:, samples[1]])
+        for t in (2, 3):
+            for h, cols in enumerate(samples):
+                project(val_ps[t][:, cols], w2_codes[t], w2_sc[t], h)
+        s_ps = [ps.tile([P, S], F32, name="s_ps%d" % t) for t in range(PACK)]
+        bg_all = placed("bg_all", [P, PACK, V], F32, BG_AT)
+        for t in range(PACK):
+            nc.sync.dma_start(bg_all[:, t, :], bg_rows[t])
+        w3_raw = placed("w3_raw", [P, PACK, N], F32, W2_AT + 4)
         for t in range(PACK):
             nc.sync.dma_start(w3_raw[:, t, :], w3_rows[t])
 
@@ -122,14 +135,15 @@ def tile_picked_nerfvol_none_p_kernel(tc, x_words, x_scales, w1, w2, bg, w3, off
         groups = ((0, 1), (1, 3), (3, 4))
         w1_bf = [tile("w1_bf%d" % t0, [P, (t1 - t0) * H], BF16) for t0, t1 in groups]
 
-        def w1_round(n, c):
+        def w1_round(n, c, copy=nc.vector.tensor_copy):
             t0, t1 = groups[n]
             dst = w1_bf[n][:].rearrange("p (t a r j) -> p a t j r", t=t1 - t0, r=RUN, j=PACK)[:, :, :, halves(PACK)[c]]
             src = w1_raw[c][:].rearrange("p j (a t r) -> p a t j r", t=PACK, r=RUN)
-            nc.vector.tensor_copy(dst, src[:, :, t0:t1])
+            copy(dst, src[:, :, t0:t1])
 
         for n in range(3):
             w1_round(n, 0)
+        nc.scalar.copy(val[1][:, samples[1]], val_ps[1][:, samples[1]])
         w1_round(0, 1)
         w1_round(1, 1)
         quantise(w1_codes[0], w1_sc[0], w1_bf[0])
@@ -138,9 +152,9 @@ def tile_picked_nerfvol_none_p_kernel(tc, x_words, x_scales, w1, w2, bg, w3, off
             quantise(w1_codes[t], w1_sc[t], w1_bf[1][:, (t - 1) * H : t * H])
         quantise(w1_codes[3], w1_sc[3], w1_bf[2])
         for t in range(PACK):
-            project(s_ps[t], w1_codes[t], w1_sc[t])
+            for h, cols in enumerate(samples):
+                project(s_ps[t][:, cols], w1_codes[t], w1_sc[t], h)
 
-        val = [placed("val%d" % t, [P, S], F32, VAL_AT + 2 * t) for t in range(PACK)]
         dens = tiles("dens", [P, S], F32)
         e2 = tiles("e2_", [P, V], F32)
         d1_all = tile("d1", [P, PACK, V], F32)
@@ -173,7 +187,7 @@ def tile_picked_nerfvol_none_p_kernel(tc, x_words, x_scales, w1, w2, bg, w3, off
         def near_share(ts, rays):
             nc.vector.scalar_tensor_tensor(u1[:, ts, rays], e1_all[:, ts, rays], one[:], d1_all[:, ts, rays], ALU.subtract, ALU.mult)
 
-        for t in range(PACK):
+        for t in (2, 3):
             nc.scalar.copy(val[t][:], val_ps[t][:])
         for t in range(PACK):
             far_contrast(t)

@@ -219,48 +219,45 @@ def tile_picked_nerfvol_none_p_kernel(tc, x_words, x_scales, w1, w2, bg, w3, off
         near_share(slice(3, 4), first)
         near_share(slice(0, 4), second)
 
-        z_bf = [tile("z_bf0", [P, V // 2 * PACK], BF16), tile("z_bf1", [P, V // 2 * PACK], BF16)]
-        z_codes = tiles("z_codes", [P, V // 2], U32, 2)
-        z_sc = tiles("z_sc", [P, V // 2], U8, 2)
+        z_bf = tile("z_bf", [P, V * PACK], BF16)
+        z_codes = tile("z_codes", [P, V], U32)
+        z_sc = tile("z_sc", [P, V], U8)
 
         def blend(h):
             rays = halves(V)[h]
-            z_view, behind_view = weave(z_bf[h][:], behind[:, :, rays])
-            z_view, u1_view = weave(z_bf[h][:], u1[:, :, rays])
+            z_view, behind_view = weave(z_bf[:, halves(V * PACK)[h]], behind[:, :, rays])
+            z_view, u1_view = weave(z_bf[:, halves(V * PACK)[h]], u1[:, :, rays])
             nc.vector.tensor_tensor(z_view, behind_view, u1_view, ALU.subtract)
 
         w3_codes[0] = placed("w3_codes0", [P, N // 2], U32, U2_AT - 2)
         blend(0)
         blend(1)
         quantise(w3_codes[0], w3_sc[0], w3_bf[0])
-        quantise(z_codes[0], z_sc[0], z_bf[0])
+        quantise(z_codes, z_sc, z_bf)
         quantise(w3_codes[1], w3_sc[1], w3_bf[1])
-        quantise(z_codes[1], z_sc[1], z_bf[1])
-        out_rows = out.rearrange("(u p) v -> p u v", p=P)
+        out_rows = out.rearrange("(u p) v -> u p v", p=P)
 
-        def product(dst, u, h):
+        def product(dst, u, rays):
             cols = halves(N // 2)[u % 2]
             nc.tensor.matmul_mx(
                 out=dst,
                 lhsT=w3_codes[u // 2][:, cols].bitcast(FP8X4),
                 lhsT_scale=w3_sc[u // 2][:, cols],
-                rhs=z_codes[h][:].bitcast(FP8X4),
-                rhs_scale=z_sc[h][:],
+                rhs=z_codes[:, rays].bitcast(FP8X4),
+                rhs_scale=z_sc[:, rays],
                 start=True,
                 stop=True,
             )
 
-        for h, rays in enumerate(halves(V)):
-            for g, empty in enumerate((nc.scalar.copy, nc.vector.tensor_copy)):
-                res = tile("res%d%d" % (h, g), [P, 2, V // 2], F32)
-                if (h, g) == (1, 1):
-                    for n in range(2):
-                        acc = ps.tile([P, V // 2], F32, name="s_ps%d" % n)
-                        product(acc[:], 2 * g + n, h)
-                        empty(res[:, n, :], acc[:])
-                else:
-                    acc = ps.tile([P, 2, V // 2], F32, name="val_ps%d" % (2 * h + g))
-                    for n in range(2):
-                        product(acc[:, n, :], 2 * g + n, h)
-                    empty(res[:], acc[:])
-                nc.sync.dma_start(out_rows[:, 2 * g : 2 * g + 2, rays], res[:])
+        for u in range(PACK):
+            res = tile("res%d" % u, [P, V], F32)
+            if u < PACK - 1:
+                acc = ps.tile([P, V], F32, name="val_ps%d" % u)
+                product(acc[:], u, slice(0, V))
+                (nc.scalar.copy, nc.vector.tensor_copy)[u % 2](res[:], acc[:])
+            else:
+                for h, rays in enumerate(halves(V)):
+                    acc = ps.tile([P, V // 2], F32, name="s_ps%d" % h)
+                    product(acc[:], u, rays)
+                    nc.vector.tensor_copy(res[:, rays], acc[:])
+            nc.sync.dma_start(out_rows[u], res[:])

@@ -231,9 +231,11 @@ def tile_picked_nerfvol_none_p_kernel(tc, x_words, x_scales, w1, w2, bg, w3, off
 
         w3_codes[0] = placed("w3_codes0", [P, N // 2], U32, U2_AT - 2)
         blend(0)
+        quantise(w3_codes[0][:, :P], w3_sc[0][:, :P], w3_bf[0][:, : P * PACK])
         blend(1)
-        quantise(w3_codes[0], w3_sc[0], w3_bf[0])
-        quantise(z_codes, z_sc, z_bf)
+        for h, rays in enumerate(halves(V)):
+            quantise(z_codes[:, rays], z_sc[:, rays], z_bf[:, halves(V * PACK)[h]])
+        quantise(w3_codes[0][:, P:], w3_sc[0][:, P:], w3_bf[0][:, P * PACK :])
         quantise(w3_codes[1], w3_sc[1], w3_bf[1])
         out_rows = out.rearrange("(u p) v -> u p v", p=P)
 
@@ -251,13 +253,13 @@ def tile_picked_nerfvol_none_p_kernel(tc, x_words, x_scales, w1, w2, bg, w3, off
 
         for u in range(PACK):
             res = tile("res%d" % u, [P, V], F32)
-            if u < PACK - 1:
+            if 0 < u < PACK - 1:
                 acc = ps.tile([P, V], F32, name="val_ps%d" % u)
                 product(acc[:], u, slice(0, V))
                 (nc.scalar.copy, nc.vector.tensor_copy)[u % 2](res[:], acc[:])
             else:
                 for h, rays in enumerate(halves(V)):
-                    acc = ps.tile([P, V // 2], F32, name="s_ps%d" % h)
+                    acc = ps.tile([P, V // 2], F32, name="s_ps%d" % (h if u else 2 + h))
                     product(acc[:], u, rays)
-                    nc.vector.tensor_copy(res[:, rays], acc[:])
+                    (nc.vector.tensor_copy if u else nc.scalar.copy)(res[:, rays], acc[:])
             nc.sync.dma_start(out_rows[u], res[:])

@@ -15,9 +15,19 @@ RUN = 4
 GROUP = 16
 QUADRANT = 32
 SCALE_ROWS = 4
-SCALES_AT = P - K // QUADRANT
-W2_AT, BG_AT, U2_AT, VAL_AT = 0, 0, 20, 24
+SCALES_FROM = P - K // 32
 FLOPS = 2 * (2 * K * H * S + H * N * V)
+
+W2_AT = 0
+W1_AT = (8, 12)
+SCALES_AT = 11
+BG_AT = 0
+W3_AT = 4
+U2_AT = 20
+E1_AT = 18
+W3_CODES_AT = 18
+VAL_AT = 24
+U1_AT = 26
 
 
 def halves(n):
@@ -38,31 +48,47 @@ def tile_picked_nerfvol_none_p_kernel(tc, x_words, x_scales, w1, w2, bg, w3, off
         def tiles(name, shape, dtype, count=PACK):
             return [tile("%s%d" % (name, n), shape, dtype) for n in range(count)]
 
+        def placed(name, shape, dtype, kib):
+            return shared.tile(shape, dtype, name=name, offset=kib * 1024, align_bytes=64)
+
+        def val_bank(t, columns):
+            return ps.tile([P, columns], F32, name="val_ps%d" % t)
+
+        def s_bank(t, columns):
+            return ps.tile([P, columns], F32, name="s_ps%d" % t)
+
         def weave(dst, src):
             return dst.rearrange("p (c i t) -> p c t i", i=RUN, t=PACK), src.rearrange("p t (c i) -> p c t i", i=RUN)
 
         def quantise(codes, scale_bytes, rounded):
-            nc.vector.quantize_mx(out=codes[:].bitcast(FP8X4), scales=scale_bytes[:], in_=rounded[:])
+            nc.vector.quantize_mx(out=codes.bitcast(FP8X4), scales=scale_bytes, in_=rounded)
+
+        def multiply(dst, lhs_codes, lhs_scales, rhs_codes, rhs_scales):
+            nc.tensor.matmul_mx(
+                out=dst,
+                lhsT=lhs_codes.bitcast(FP8X4),
+                lhsT_scale=lhs_scales,
+                rhs=rhs_codes.bitcast(FP8X4),
+                rhs_scale=rhs_scales,
+                start=True,
+                stop=True,
+            )
 
         offs_t = lists.tile([P, S // GROUP], U16, name="offs_t")
         p1_t = lists.tile([P, V // GROUP], U16, name="p1_t")
         p2_t = lists.tile([P, V // GROUP], U16, name="p2_t")
-
-        def placed(name, shape, dtype, kib):
-            return shared.tile(shape, dtype, name=name, offset=kib * 1024, align_bytes=64)
-
         words = tile("words", [P, T], U32)
-        scales = placed("scales", [P, T], U8, W2_AT + 11)
+        scales = placed("scales", [P, T], U8, SCALES_AT)
         x_bytes = tile("x_bytes", [P, S], U8)
         zero = tile("zero", [P, 1], F32)
         one = tile("one", [P, 1], F32)
 
         nc.vector.memset(zero[:], 0.0)
-        nc.vector.memset(scales[:SCALES_AT, :].bitcast(I32), 0)
+        nc.vector.memset(scales[:SCALES_FROM, :].bitcast(I32), 0)
         nc.vector.memset(x_bytes[:].bitcast(I32), 0)
         w2_raw = placed("w2_raw", [P, PACK, H], F32, W2_AT)
         nc.sync.dma_start(offs_t[:], offs)
-        nc.scalar.dma_start(scales[SCALES_AT:, :].bitcast(I32), x_scales[0].bitcast(I32))
+        nc.scalar.dma_start(scales[SCALES_FROM:, :].bitcast(I32), x_scales[0].bitcast(I32))
         nc.sync.dma_start(w2_raw[:], w2.rearrange("(p j) c -> p j c", j=PACK))
         nc.sync.dma_start(p2_t[:], p2)
         nc.sync.dma_start(words[:].bitcast(I32), x_words[0].rearrange("p n j -> p (n j)").bitcast(I32))
@@ -73,46 +99,37 @@ def tile_picked_nerfvol_none_p_kernel(tc, x_words, x_scales, w1, w2, bg, w3, off
         x_codes = tiles("x_codes", [P, S // 2], U32, 2)
         samples = halves(S)
         nc.vector.tensor_copy(picked_scales[:], scales[:].indirect(offs_t[:]))
-        for q in range(P // QUADRANT):
-            rows = slice(SCALES_AT + SCALE_ROWS * q, SCALES_AT + SCALE_ROWS * (q + 1))
-            nc.sync.dma_start(x_bytes[QUADRANT * q : QUADRANT * q + SCALE_ROWS, :].bitcast(I32), picked_scales[rows, :].bitcast(I32))
-        w1_raw = [placed("w1_raw%d" % c, [P, PACK // 2, H], F32, at) for c, at in enumerate((W2_AT + 8, W2_AT + 12))]
-        w1_cols = w1.rearrange("(p j) c -> p j c", j=PACK)
-        for c, rows in enumerate(halves(PACK)):
-            nc.sync.dma_start(w1_raw[c][:], w1_cols[:, rows])
-        val_ps = [ps.tile([P, S], F32, name="val_ps%d" % t) for t in range(PACK)]
-
-        def project(bank, codes, scale_bytes, h):
-            cols = samples[h]
-            nc.tensor.matmul_mx(
-                out=bank,
-                lhsT=codes[:].bitcast(FP8X4),
-                lhsT_scale=scale_bytes[:],
-                rhs=x_codes[h][:].bitcast(FP8X4),
-                rhs_scale=x_bytes[:, cols],
-                start=True,
-                stop=True,
+        for quadrant in range(P // QUADRANT):
+            src = SCALES_FROM + SCALE_ROWS * quadrant
+            dst = QUADRANT * quadrant
+            nc.sync.dma_start(
+                x_bytes[dst : dst + SCALE_ROWS, :].bitcast(I32), picked_scales[src : src + SCALE_ROWS, :].bitcast(I32)
             )
+        w1_raw = [placed("w1_raw%d" % part, [P, PACK // 2, H], F32, at) for part, at in enumerate(W1_AT)]
+        for part, js in enumerate(halves(PACK)):
+            nc.sync.dma_start(w1_raw[part][:], w1.rearrange("(p j) c -> p j c", j=PACK)[:, js])
+        val_ps = [val_bank(t, S) for t in range(PACK)]
 
-        def round_tiles(copy, dst, raw, t0, t1):
-            dst = dst.rearrange("p (t a r j) -> p a t j r", t=t1 - t0, r=RUN, j=PACK)
-            src = raw[:].rearrange("p j (a t r) -> p a t j r", t=PACK, r=RUN)
-            copy(dst, src[:, :, t0:t1])
+        def project(dst, codes, scale_bytes, h):
+            multiply(dst, codes[:], scale_bytes[:], x_codes[h][:], x_bytes[:, samples[h]])
 
-        bg_rows = bg.rearrange("(a t r) v -> t a r v", t=PACK, r=RUN)
-        w3_rows = w3.rearrange("(a t r) m -> t a r m", t=PACK, r=RUN)
+        def rounding_views(dst, raw, t0, t1):
+            return (
+                dst.rearrange("p (t a r j) -> p a t j r", t=t1 - t0, r=RUN, j=PACK),
+                raw.rearrange("p j (a t r) -> p a t j r", t=PACK, r=RUN)[:, :, t0:t1],
+            )
 
         w2_bf = tiles("w2_bf", [P, H], BF16)
         w2_codes = tiles("w2_codes", [P, P], U32)
         w2_sc = tiles("w2_sc", [P, P], U8)
         for t in range(PACK):
-            round_tiles(nc.vector.tensor_copy if t % 2 == 0 else nc.scalar.copy, w2_bf[t][:], w2_raw, t, t + 1)
+            (nc.vector.tensor_copy, nc.scalar.copy)[t % 2](*rounding_views(w2_bf[t][:], w2_raw[:], t, t + 1))
         for t in range(PACK):
-            quantise(w2_codes[t], w2_sc[t], w2_bf[t])
-        for h, cols in enumerate(samples):
+            quantise(w2_codes[t][:], w2_sc[t][:], w2_bf[t][:])
+        for h in range(2):
             nc.vector.tensor_copy(x_codes[h][:], words[:].indirect(offs_t[:, halves(S // GROUP)[h]]))
         val = [placed("val%d" % t, [P, S], F32, VAL_AT + 2 * t) for t in range(PACK)]
-        early = [ps.tile([P, S // 2], F32, name="s_ps%d" % (2 + t)) for t in range(2)]
+        early = [s_bank(2 + t, S // 2) for t in range(2)]
         for t in range(2):
             project(early[t][:], w2_codes[t], w2_sc[t], 0)
             nc.scalar.copy(val[t][:, samples[0]], early[t][:])
@@ -122,55 +139,52 @@ def tile_picked_nerfvol_none_p_kernel(tc, x_words, x_scales, w1, w2, bg, w3, off
         for t in (2, 3):
             for h, cols in enumerate(samples):
                 project(val_ps[t][:, cols], w2_codes[t], w2_sc[t], h)
-        s_ps = [ps.tile([P, S], F32, name="s_ps%d" % t) for t in range(PACK)]
+        s_ps = [s_bank(t, S) for t in range(PACK)]
+
+        bg_rows = bg.rearrange("(a t r) v -> t a r v", t=PACK, r=RUN)
+        w3_rows = w3.rearrange("(a t r) m -> t a r m", t=PACK, r=RUN)
         bg_all = placed("bg_all", [P, PACK, V], F32, BG_AT)
         for t in range(PACK):
             nc.sync.dma_start(bg_all[:, t, :], bg_rows[t])
-        w3_raw = placed("w3_raw", [P, PACK, N], F32, W2_AT + 4)
+        w3_raw = placed("w3_raw", [P, PACK, N], F32, W3_AT)
         for t in range(PACK):
             nc.sync.dma_start(w3_raw[:, t, :], w3_rows[t])
 
         w1_codes = tiles("w1_codes", [P, P], U32)
         w1_sc = tiles("w1_sc", [P, P], U8)
-        groups = ((0, 1), (1, 3), (3, 4))
-        w1_bf = [tile("w1_bf%d" % t0, [P, (t1 - t0) * H], BF16) for t0, t1 in groups]
+        spans = ((0, 1), (1, 3), (3, 4))
+        w1_bf = [tile("w1_bf%d" % t0, [P, (t1 - t0) * H], BF16) for t0, t1 in spans]
 
-        def w1_round(n, c, copy=nc.vector.tensor_copy):
-            t0, t1 = groups[n]
-            dst = w1_bf[n][:].rearrange("p (t a r j) -> p a t j r", t=t1 - t0, r=RUN, j=PACK)[:, :, :, halves(PACK)[c]]
-            src = w1_raw[c][:].rearrange("p j (a t r) -> p a t j r", t=PACK, r=RUN)
-            copy(dst, src[:, :, t0:t1])
+        def w1_round(span, part):
+            dst, src = rounding_views(w1_bf[span][:], w1_raw[part][:], *spans[span])
+            nc.vector.tensor_copy(dst[:, :, :, halves(PACK)[part]], src)
 
-        for n in range(3):
-            w1_round(n, 0)
+        for span in range(len(spans)):
+            w1_round(span, 0)
         nc.scalar.copy(val[1][:, samples[1]], val_ps[1][:, samples[1]])
         w1_round(0, 1)
         w1_round(1, 1)
-        quantise(w1_codes[0], w1_sc[0], w1_bf[0])
+        quantise(w1_codes[0][:], w1_sc[0][:], w1_bf[0][:])
         w1_round(2, 1)
         for t in (1, 2):
-            quantise(w1_codes[t], w1_sc[t], w1_bf[1][:, (t - 1) * H : t * H])
-        quantise(w1_codes[3], w1_sc[3], w1_bf[2])
+            quantise(w1_codes[t][:], w1_sc[t][:], w1_bf[1][:, (t - 1) * H : t * H])
+        quantise(w1_codes[3][:], w1_sc[3][:], w1_bf[2][:])
         for t in range(PACK):
             for h, cols in enumerate(samples):
                 project(s_ps[t][:, cols], w1_codes[t], w1_sc[t], h)
 
         dens = tiles("dens", [P, S], F32)
         e2 = tiles("e2_", [P, V], F32)
-        d1_all = tile("d1", [P, PACK, V], F32)
-        d1 = [d1_all[:, t, :] for t in range(PACK)]
+        d1 = tile("d1", [P, PACK, V], F32)
         d2 = tiles("d2_", [P, V], F32)
         u2 = [placed("u2_%d" % t, [P, V], F32, U2_AT + t) for t in range(PACK)]
         behind = tile("behind", [P, PACK, V], F32)
         w3_bf = [tile("w3_bf%d" % g, [P, N * PACK // 2], BF16, "dens%d" % g) for g in range(2)]
-        w3_codes = [None, tile("w3_codes1", [P, N // 2], U32)]
+        w3_codes_last = tile("w3_codes1", [P, N // 2], U32)
         w3_sc = tiles("w3_sc", [P, N // 2], U8, 2)
 
-        def density(t):
-            nc.scalar.activation(dens[t][:], s_ps[t][:], ACT.Relu)
-
-        def transmittance(e, list_t, t):
-            nc.scalar.activation(e[t][:], dens[t][:].indirect(list_t[:]), ACT.Exp, scale=-1.0)
+        def transmittance(dst, list_t, t):
+            nc.scalar.activation(dst, dens[t][:].indirect(list_t[:]), ACT.Exp, scale=-1.0)
 
         def far_contrast(t):
             nc.vector.tensor_tensor(d2[t][:], val[t][:].indirect(p2_t[:]), bg_all[:, t, :], ALU.subtract)
@@ -182,10 +196,7 @@ def tile_picked_nerfvol_none_p_kernel(tc, x_words, x_scales, w1, w2, bg, w3, off
             nc.vector.tensor_tensor(behind[:, t, :], bg_all[:, t, :], u2[t][:], ALU.subtract)
 
         def near_contrast(t):
-            nc.vector.tensor_tensor(d1[t][:], val[t][:].indirect(p1_t[:]), behind[:, t, :], ALU.subtract)
-
-        def near_share(ts, rays):
-            nc.vector.scalar_tensor_tensor(u1[:, ts, rays], e1_all[:, ts, rays], one[:], d1_all[:, ts, rays], ALU.subtract, ALU.mult)
+            nc.vector.tensor_tensor(d1[:, t, :], val[t][:].indirect(p1_t[:]), behind[:, t, :], ALU.subtract)
 
         for t in (2, 3):
             nc.scalar.copy(val[t][:], val_ps[t][:])
@@ -194,9 +205,9 @@ def tile_picked_nerfvol_none_p_kernel(tc, x_words, x_scales, w1, w2, bg, w3, off
 
         def far_lookups(pair):
             for t in pair:
-                density(t)
+                nc.scalar.activation(dens[t][:], s_ps[t][:], ACT.Relu)
             for t in pair:
-                transmittance(e2, p2_t, t)
+                transmittance(e2[t][:], p2_t, t)
 
         def far_steps(pair):
             for step in (far_share, far_blend, near_contrast):
@@ -206,60 +217,52 @@ def tile_picked_nerfvol_none_p_kernel(tc, x_words, x_scales, w1, w2, bg, w3, off
         far_lookups((0, 1))
         far_steps((0, 1))
         far_lookups((2, 3))
-        e1_all = placed("e1", [P, PACK, V], F32, U2_AT - 2)
-        e1 = [e1_all[:, t, :] for t in range(PACK)]
+        e1 = placed("e1", [P, PACK, V], F32, E1_AT)
         for t in range(PACK):
-            transmittance(e1, p1_t, t)
-        for g, cols in enumerate(halves(N)):
-            nc.scalar.copy(*weave(w3_bf[g][:], w3_raw[:, :, cols]))
+            transmittance(e1[:, t, :], p1_t, t)
+        nc.scalar.copy(*weave(w3_bf[0][:], w3_raw[:, :, : N // 2]))
+        for u in (2, 3):
+            nc.scalar.copy(*weave(w3_bf[1][:, halves(N * PACK // 2)[u % 2]], w3_raw[:, :, u * P : (u + 1) * P]))
         far_steps((2, 3))
-        u1 = placed("u1", [P, PACK, V], F32, VAL_AT + 2)
+
+        u1 = placed("u1", [P, PACK, V], F32, U1_AT)
         first, second = halves(V)
-        near_share(slice(0, 3), first)
-        near_share(slice(3, 4), first)
-        near_share(slice(0, 4), second)
+        for ts, rays in ((slice(0, 3), first), (slice(3, 4), first), (slice(0, 4), second)):
+            nc.vector.scalar_tensor_tensor(u1[:, ts, rays], e1[:, ts, rays], one[:], d1[:, ts, rays], ALU.subtract, ALU.mult)
 
         z_bf = tile("z_bf", [P, V * PACK], BF16)
         z_codes = tile("z_codes", [P, V], U32)
         z_sc = tile("z_sc", [P, V], U8)
-
-        def blend(h):
-            rays = halves(V)[h]
-            z_view, behind_view = weave(z_bf[:, halves(V * PACK)[h]], behind[:, :, rays])
-            z_view, u1_view = weave(z_bf[:, halves(V * PACK)[h]], u1[:, :, rays])
+        z_halves = [z_bf[:, cols] for cols in halves(V * PACK)]
+        w3_codes = [placed("w3_codes0", [P, N // 2], U32, W3_CODES_AT), w3_codes_last]
+        for z_half, rays in zip(z_halves, (first, second)):
+            z_view, behind_view = weave(z_half, behind[:, :, rays])
+            z_view, u1_view = weave(z_half, u1[:, :, rays])
             nc.vector.tensor_tensor(z_view, behind_view, u1_view, ALU.subtract)
 
-        w3_codes[0] = placed("w3_codes0", [P, N // 2], U32, U2_AT - 2)
-        blend(0)
+        quantise(z_codes[:, first], z_sc[:, first], z_halves[0])
         quantise(w3_codes[0][:, :P], w3_sc[0][:, :P], w3_bf[0][:, : P * PACK])
-        blend(1)
-        for h, rays in enumerate(halves(V)):
-            quantise(z_codes[:, rays], z_sc[:, rays], z_bf[:, halves(V * PACK)[h]])
+        quantise(z_codes[:, second], z_sc[:, second], z_halves[1])
         quantise(w3_codes[0][:, P:], w3_sc[0][:, P:], w3_bf[0][:, P * PACK :])
-        quantise(w3_codes[1], w3_sc[1], w3_bf[1])
+        for cols, rounded in zip(halves(N // 2), halves(N * PACK // 2)):
+            quantise(w3_codes[1][:, cols], w3_sc[1][:, cols], w3_bf[1][:, rounded])
+
         out_rows = out.rearrange("(u p) v -> u p v", p=P)
 
         def product(dst, u, rays):
             cols = halves(N // 2)[u % 2]
-            nc.tensor.matmul_mx(
-                out=dst,
-                lhsT=w3_codes[u // 2][:, cols].bitcast(FP8X4),
-                lhsT_scale=w3_sc[u // 2][:, cols],
-                rhs=z_codes[:, rays].bitcast(FP8X4),
-                rhs_scale=z_sc[:, rays],
-                start=True,
-                stop=True,
-            )
+            multiply(dst, w3_codes[u // 2][:, cols], w3_sc[u // 2][:, cols], z_codes[:, rays], z_sc[:, rays])
 
         for u in range(PACK):
             res = tile("res%d" % u, [P, V], F32)
-            if 0 < u < PACK - 1:
-                acc = ps.tile([P, V], F32, name="val_ps%d" % u)
-                product(acc[:], u, slice(0, V))
-                (nc.scalar.copy, nc.vector.tensor_copy)[u % 2](res[:], acc[:])
-            else:
-                for h, rays in enumerate(halves(V)):
-                    acc = ps.tile([P, V // 2], F32, name="s_ps%d" % (h if u else 2 + h))
+            empty = (nc.scalar.copy, nc.vector.tensor_copy)[u % 2]
+            if u in (0, PACK - 1):
+                for h, rays in enumerate((first, second)):
+                    acc = s_bank(2 + h if u == 0 else h, V // 2)
                     product(acc[:], u, rays)
-                    (nc.vector.tensor_copy if u else nc.scalar.copy)(res[:, rays], acc[:])
+                    empty(res[:, rays], acc[:])
+            else:
+                acc = val_bank(u, V)
+                product(acc[:], u, slice(0, V))
+                empty(res[:], acc[:])
             nc.sync.dma_start(out_rows[u], res[:])

@@ -152,7 +152,7 @@ def tile_picked_nerfvol_none_p_kernel(tc, x_words, x_scales, w1, w2, bg, w3, off
 
         w1_codes = tiles("w1_codes", [P, P], U32)
         w1_sc = tiles("w1_sc", [P, P], U8)
-        spans = ((0, 1), (1, 3), (3, 4))
+        spans = ((0, 1), (1, 2), (2, 4))
         w1_bf = [tile("w1_bf%d" % t0, [P, (t1 - t0) * H], BF16) for t0, t1 in spans]
 
         def w1_round(span, part):
@@ -166,9 +166,9 @@ def tile_picked_nerfvol_none_p_kernel(tc, x_words, x_scales, w1, w2, bg, w3, off
         w1_round(1, 1)
         quantise(w1_codes[0][:], w1_sc[0][:], w1_bf[0][:])
         w1_round(2, 1)
-        for t in (1, 2):
-            quantise(w1_codes[t][:], w1_sc[t][:], w1_bf[1][:, (t - 1) * H : t * H])
-        quantise(w1_codes[3][:], w1_sc[3][:], w1_bf[2][:])
+        quantise(w1_codes[1][:], w1_sc[1][:], w1_bf[1][:])
+        for t in (2, 3):
+            quantise(w1_codes[t][:], w1_sc[t][:], w1_bf[2][:, (t - 2) * H : (t - 1) * H])
         for t in range(PACK):
             for h, cols in enumerate(samples):
                 project(s_ps[t][:, cols], w1_codes[t], w1_sc[t], h)

@@ -18,16 +18,19 @@ SCALE_ROWS = 4
 SCALES_FROM = P - K // 32
 FLOPS = 2 * (2 * K * H * S + H * N * V)
 
-W2_AT = 0
-W1_AT = (8, 12)
-SCALES_AT = 11
-BG_AT = 0
-W3_AT = 4
-U2_AT = 20
-E1_AT = 18
-W3_CODES_AT = 18
-VAL_AT = 24
-U1_AT = 26
+W1_AT = 2
+W2_AT = (10, 14)
+SCALES_AT = 13
+BG_AT = 4
+W3_AT = 10
+DENS_AT = (48, 50)
+FETCHED_AT = (6, 48)
+E_AT = 20
+W3_CODES_AT = (26, 56)
+A_AT = 28
+W3_BF_AT = (32, 34)
+M2_AT = 40
+M1_AT = 56
 
 
 def halves(n):
@@ -51,11 +54,8 @@ def tile_picked_nerfvol_none_p_kernel(tc, x_words, x_scales, w1, w2, bg, w3, off
         def placed(name, shape, dtype, kib):
             return shared.tile(shape, dtype, name=name, offset=kib * 1024, align_bytes=64)
 
-        def val_bank(t, columns):
-            return ps.tile([P, columns], F32, name="val_ps%d" % t)
-
-        def s_bank(t, columns):
-            return ps.tile([P, columns], F32, name="s_ps%d" % t)
+        def bank(n, columns):
+            return ps.tile([P, columns], F32, name="bank%d" % n)
 
         def weave(dst, src):
             return dst.rearrange("p (c i t) -> p c t i", i=RUN, t=PACK), src.rearrange("p t (c i) -> p c t i", i=RUN)
@@ -86,10 +86,10 @@ def tile_picked_nerfvol_none_p_kernel(tc, x_words, x_scales, w1, w2, bg, w3, off
         nc.vector.memset(zero[:], 0.0)
         nc.vector.memset(scales[:SCALES_FROM, :].bitcast(I32), 0)
         nc.vector.memset(x_bytes[:].bitcast(I32), 0)
-        w2_raw = placed("w2_raw", [P, PACK, H], F32, W2_AT)
+        w1_raw = placed("w1_raw", [P, PACK, H], F32, W1_AT)
         nc.sync.dma_start(offs_t[:], offs)
         nc.scalar.dma_start(scales[SCALES_FROM:, :].bitcast(I32), x_scales[0].bitcast(I32))
-        nc.sync.dma_start(w2_raw[:], w2.rearrange("(p j) c -> p j c", j=PACK))
+        nc.sync.dma_start(w1_raw[:], w1.rearrange("(p j) c -> p j c", j=PACK))
         nc.sync.dma_start(p2_t[:], p2)
         nc.sync.dma_start(words[:].bitcast(I32), x_words[0].rearrange("p n j -> p (n j)").bitcast(I32))
         nc.sync.dma_start(p1_t[:], p1)
@@ -105,10 +105,9 @@ def tile_picked_nerfvol_none_p_kernel(tc, x_words, x_scales, w1, w2, bg, w3, off
             nc.sync.dma_start(
                 x_bytes[dst : dst + SCALE_ROWS, :].bitcast(I32), picked_scales[src : src + SCALE_ROWS, :].bitcast(I32)
             )
-        w1_raw = [placed("w1_raw%d" % part, [P, PACK // 2, H], F32, at) for part, at in enumerate(W1_AT)]
+        w2_raw = [placed("w2_raw%d" % part, [P, PACK // 2, H], F32, at) for part, at in enumerate(W2_AT)]
         for part, js in enumerate(halves(PACK)):
-            nc.sync.dma_start(w1_raw[part][:], w1.rearrange("(p j) c -> p j c", j=PACK)[:, js])
-        val_ps = [val_bank(t, S) for t in range(PACK)]
+            nc.sync.dma_start(w2_raw[part][:], w2.rearrange("(p j) c -> p j c", j=PACK)[:, js])
 
         def project(dst, codes, scale_bytes, h):
             multiply(dst, codes[:], scale_bytes[:], x_codes[h][:], x_bytes[:, samples[h]])
@@ -119,27 +118,32 @@ def tile_picked_nerfvol_none_p_kernel(tc, x_words, x_scales, w1, w2, bg, w3, off
                 raw.rearrange("p j (a t r) -> p a t j r", t=PACK, r=RUN)[:, :, t0:t1],
             )
 
-        w2_bf = tiles("w2_bf", [P, H], BF16)
-        w2_codes = tiles("w2_codes", [P, P], U32)
-        w2_sc = tiles("w2_sc", [P, P], U8)
+        w1_bf = tiles("w1_bf", [P, H], BF16)
+        w1_codes = tiles("w1_codes", [P, P], U32)
+        w1_sc = tiles("w1_sc", [P, P], U8)
         for t in range(PACK):
-            (nc.vector.tensor_copy, nc.scalar.copy)[t % 2](*rounding_views(w2_bf[t][:], w2_raw[:], t, t + 1))
+            (nc.vector.tensor_copy, nc.scalar.copy)[t % 2](*rounding_views(w1_bf[t][:], w1_raw[:], t, t + 1))
         for t in range(PACK):
-            quantise(w2_codes[t][:], w2_sc[t][:], w2_bf[t][:])
+            quantise(w1_codes[t][:], w1_sc[t][:], w1_bf[t][:])
         for h in range(2):
             nc.vector.tensor_copy(x_codes[h][:], words[:].indirect(offs_t[:, halves(S // GROUP)[h]]))
-        val = [placed("val%d" % t, [P, S], F32, VAL_AT + 2 * t) for t in range(PACK)]
-        early = [s_bank(2 + t, S // 2) for t in range(2)]
+        e = [placed("e%d" % t, [P, S], F32, E_AT + 2 * t) for t in range(PACK)]
+        dens = [placed("dens%d" % t, [P, S], F32, DENS_AT[t]) for t in range(2)]
+        for h, cols in enumerate(samples):
+            for t in range(2):
+                acc = bank(2 * h + t, S // 2)
+                project(acc[:], w1_codes[t], w1_sc[t], h)
+                nc.scalar.activation(dens[t][:, cols], acc[:], ACT.Relu)
         for t in range(2):
-            project(early[t][:], w2_codes[t], w2_sc[t], 0)
-            nc.scalar.copy(val[t][:, samples[0]], early[t][:])
+            nc.scalar.activation(e[t][:], dens[t][:], ACT.Exp, scale=-1.0)
+        dens = [placed("dens%d" % (2 + t), [P, S], F32, DENS_AT[t]) for t in range(2)]
         for t in range(2):
-            project(val_ps[t][:, samples[1]], w2_codes[t], w2_sc[t], 1)
-        nc.scalar.copy(val[0][:, samples[1]], val_ps[0][:, samples[1]])
-        for t in (2, 3):
+            acc = bank(4 + t, S)
             for h, cols in enumerate(samples):
-                project(val_ps[t][:, cols], w2_codes[t], w2_sc[t], h)
-        s_ps = [s_bank(t, S) for t in range(PACK)]
+                project(acc[:, cols], w1_codes[2 + t], w1_sc[2 + t], h)
+            nc.scalar.activation(dens[t][:], acc[:], ACT.Relu)
+        for t in range(2):
+            nc.scalar.activation(e[2 + t][:], dens[t][:], ACT.Exp, scale=-1.0)
 
         bg_rows = bg.rearrange("(a t r) v -> t a r v", t=PACK, r=RUN)
         w3_rows = w3.rearrange("(a t r) m -> t a r m", t=PACK, r=RUN)
@@ -150,95 +154,77 @@ def tile_picked_nerfvol_none_p_kernel(tc, x_words, x_scales, w1, w2, bg, w3, off
         for t in range(PACK):
             nc.sync.dma_start(w3_raw[:, t, :], w3_rows[t])
 
-        w1_codes = tiles("w1_codes", [P, P], U32)
-        w1_sc = tiles("w1_sc", [P, P], U8)
+        w2_codes = tiles("w2_codes", [P, P], U32)
+        w2_sc = tiles("w2_sc", [P, P], U8)
         spans = ((0, 1), (1, 2), (2, 4))
-        w1_bf = [tile("w1_bf%d" % t0, [P, (t1 - t0) * H], BF16) for t0, t1 in spans]
+        w2_bf = [tile("w2_bf%d" % t0, [P, (t1 - t0) * H], BF16) for t0, t1 in spans]
 
-        def w1_round(span, part):
-            dst, src = rounding_views(w1_bf[span][:], w1_raw[part][:], *spans[span])
+        def w2_round(span, part):
+            dst, src = rounding_views(w2_bf[span][:], w2_raw[part][:], *spans[span])
             nc.vector.tensor_copy(dst[:, :, :, halves(PACK)[part]], src)
 
         for span in range(len(spans)):
-            w1_round(span, 0)
-        nc.scalar.copy(val[1][:, samples[1]], val_ps[1][:, samples[1]])
-        w1_round(0, 1)
-        w1_round(1, 1)
-        quantise(w1_codes[0][:], w1_sc[0][:], w1_bf[0][:])
-        w1_round(2, 1)
-        quantise(w1_codes[1][:], w1_sc[1][:], w1_bf[1][:])
+            w2_round(span, 0)
+        w2_round(0, 1)
+        w2_round(1, 1)
+        quantise(w2_codes[0][:], w2_sc[0][:], w2_bf[0][:])
+        w2_round(2, 1)
+        quantise(w2_codes[1][:], w2_sc[1][:], w2_bf[1][:])
         for t in (2, 3):
-            quantise(w1_codes[t][:], w1_sc[t][:], w1_bf[2][:, (t - 2) * H : (t - 1) * H])
+            quantise(w2_codes[t][:], w2_sc[t][:], w2_bf[2][:, (t - 2) * H : (t - 1) * H])
+        val_ps = [bank((6 + t) % 8, S) for t in range(PACK)]
         for t in range(PACK):
             for h, cols in enumerate(samples):
-                project(s_ps[t][:, cols], w1_codes[t], w1_sc[t], h)
+                project(val_ps[t][:, cols], w2_codes[t], w2_sc[t], h)
 
-        dens = tiles("dens", [P, S], F32)
-        e2 = tiles("e2_", [P, V], F32)
-        d1 = tile("d1", [P, PACK, V], F32)
-        d2 = tiles("d2_", [P, V], F32)
-        u2 = [placed("u2_%d" % t, [P, V], F32, U2_AT + t) for t in range(PACK)]
+        a = [placed("a%d" % t, [P, S], F32, A_AT + 2 * t) for t in range(PACK)]
+        m2 = [placed("m2_%d" % t, [P, V], F32, M2_AT + t) for t in range(PACK)]
+
+        def far_product(t):
+            nc.vector.tensor_tensor(m2[t][:], e[t][:].indirect(p2_t[:]), bg_all[:, t, :], ALU.mult)
+
+        def emission(t):
+            nc.vector.scalar_tensor_tensor(a[t][:], e[t][:], one[:], val_ps[t][:], ALU.subtract, ALU.mult)
+
+        for t in range(PACK):
+            for step in (far_product, emission) if t < PACK - 1 else (emission, far_product):
+                step(t)
+        a1, a2 = [placed("a%d_fetched" % (1 + n), [P, PACK, V], F32, at) for n, at in enumerate(FETCHED_AT)]
+        for dst, list_t in ((a2, p2_t), (a1, p1_t)):
+            for t in range(PACK):
+                nc.scalar.activation(dst[:, t, :], a[t][:].indirect(list_t[:]), ACT.Copy)
+
         behind = tile("behind", [P, PACK, V], F32)
-        w3_bf = [tile("w3_bf%d" % g, [P, N * PACK // 2], BF16, "dens%d" % g) for g in range(2)]
-        w3_codes_last = tile("w3_codes1", [P, N // 2], U32)
-        w3_sc = tiles("w3_sc", [P, N // 2], U8, 2)
-
-        def transmittance(dst, list_t, t):
-            nc.scalar.activation(dst, dens[t][:].indirect(list_t[:]), ACT.Exp, scale=-1.0)
-
-        def far_contrast(t):
-            nc.vector.tensor_tensor(d2[t][:], val[t][:].indirect(p2_t[:]), bg_all[:, t, :], ALU.subtract)
-
-        def far_share(t):
-            nc.vector.scalar_tensor_tensor(u2[t][:], e2[t][:], one[:], d2[t][:], ALU.subtract, ALU.mult)
+        m1 = placed("m1", [P, PACK, V], F32, M1_AT)
+        first, second = halves(V)
 
         def far_blend(t):
-            nc.vector.tensor_tensor(behind[:, t, :], bg_all[:, t, :], u2[t][:], ALU.subtract)
+            nc.vector.tensor_tensor(behind[:, t, :], m2[t][:], a2[:, t, :], ALU.subtract)
 
-        def near_contrast(t):
-            nc.vector.tensor_tensor(d1[:, t, :], val[t][:].indirect(p1_t[:]), behind[:, t, :], ALU.subtract)
+        def near_product(t, rays=slice(0, V), entries=slice(0, V // GROUP)):
+            nc.vector.tensor_tensor(m1[:, t, rays], e[t][:].indirect(p1_t[:, entries]), behind[:, t, rays], ALU.mult)
 
-        for t in (2, 3):
-            nc.scalar.copy(val[t][:], val_ps[t][:])
-        for t in range(PACK):
-            far_contrast(t)
-
-        def far_lookups(pair):
-            for t in pair:
-                nc.scalar.activation(dens[t][:], s_ps[t][:], ACT.Relu)
-            for t in pair:
-                transmittance(e2[t][:], p2_t, t)
-
-        def far_steps(pair):
-            for step in (far_share, far_blend, near_contrast):
-                for t in pair:
-                    step(t)
-
-        far_lookups((0, 1))
-        far_steps((0, 1))
-        far_lookups((2, 3))
-        e1 = placed("e1", [P, PACK, V], F32, E1_AT)
-        for t in range(PACK):
-            transmittance(e1[:, t, :], p1_t, t)
+        far_blend(0)
+        w3_bf = [placed("w3_bf%d" % g, [P, N * PACK // 2], BF16, at) for g, at in enumerate(W3_BF_AT)]
+        w3_sc = tiles("w3_sc", [P, N // 2], U8, 2)
         nc.scalar.copy(*weave(w3_bf[0][:], w3_raw[:, :, : N // 2]))
         for u in (2, 3):
             nc.scalar.copy(*weave(w3_bf[1][:, halves(N * PACK // 2)[u % 2]], w3_raw[:, :, u * P : (u + 1) * P]))
-        far_steps((2, 3))
-
-        u1 = placed("u1", [P, PACK, V], F32, U1_AT)
-        first, second = halves(V)
-        for ts, rays in ((slice(0, 3), first), (slice(3, 4), first), (slice(0, 4), second)):
-            nc.vector.scalar_tensor_tensor(u1[:, ts, rays], e1[:, ts, rays], one[:], d1[:, ts, rays], ALU.subtract, ALU.mult)
+        for t in range(1, PACK):
+            far_blend(t)
+            near_product(t - 1)
+        for rays, entries in zip(halves(V), halves(V // GROUP)):
+            near_product(PACK - 1, rays, entries)
 
         z_bf = tile("z_bf", [P, V * PACK], BF16)
         z_codes = tile("z_codes", [P, V], U32)
         z_sc = tile("z_sc", [P, V], U8)
         z_halves = [z_bf[:, cols] for cols in halves(V * PACK)]
-        w3_codes = [placed("w3_codes0", [P, N // 2], U32, W3_CODES_AT), w3_codes_last]
         for z_half, rays in zip(z_halves, (first, second)):
-            z_view, behind_view = weave(z_half, behind[:, :, rays])
-            z_view, u1_view = weave(z_half, u1[:, :, rays])
-            nc.vector.tensor_tensor(z_view, behind_view, u1_view, ALU.subtract)
+            z_view, m1_view = weave(z_half, m1[:, :, rays])
+            z_view, a1_view = weave(z_half, a1[:, :, rays])
+            nc.vector.tensor_tensor(z_view, m1_view, a1_view, ALU.subtract)
+        w3_codes = [placed("w3_codes%d" % g, [P, N // 2], U32, at) for g, at in enumerate(W3_CODES_AT)]
 
         quantise(z_codes[:, first], z_sc[:, first], z_halves[0])
         quantise(w3_codes[0][:, :P], w3_sc[0][:, :P], w3_bf[0][:, : P * PACK])
@@ -258,11 +244,11 @@ def tile_picked_nerfvol_none_p_kernel(tc, x_words, x_scales, w1, w2, bg, w3, off
             empty = (nc.scalar.copy, nc.vector.tensor_copy)[u % 2]
             if u in (0, PACK - 1):
                 for h, rays in enumerate((first, second)):
-                    acc = s_bank(2 + h if u == 0 else h, V // 2)
+                    acc = bank(2 + h if u == 0 else 6 + h, V // 2)
                     product(acc[:], u, rays)
                     empty(res[:, rays], acc[:])
             else:
-                acc = val_bank(u, V)
+                acc = bank(3 + u, V)
                 product(acc[:], u, slice(0, V))
                 empty(res[:], acc[:])
             nc.sync.dma_start(out_rows[u], res[:])

@@ -21,14 +21,15 @@ FLOPS = 2 * (2 * K * H * S + H * N * V)
 W1_AT = 2
 W2_AT = (10, 14)
 SCALES_AT = 13
-BG_AT = 4
-W3_AT = 10
+BG_AT = (3, 4, 5, 6)
+WORDS_AT = 60
+W3_AT = 60
 DENS_AT = (48, 50)
 FETCHED_AT = (6, 48)
 E_AT = 20
 W3_CODES_AT = (26, 56)
 A_AT = 28
-W3_BF_AT = (32, 34)
+W3_BF_AT = (5, 32, 34)
 M2_AT = 40
 M1_AT = 56
 
@@ -77,7 +78,7 @@ def tile_picked_nerfvol_none_p_kernel(tc, x_words, x_scales, w1, w2, bg, w3, off
         offs_t = lists.tile([P, S // GROUP], U16, name="offs_t")
         p1_t = lists.tile([P, V // GROUP], U16, name="p1_t")
         p2_t = lists.tile([P, V // GROUP], U16, name="p2_t")
-        words = tile("words", [P, T], U32)
+        words = placed("words", [P, T], U32, WORDS_AT)
         scales = placed("scales", [P, T], U8, SCALES_AT)
         x_bytes = tile("x_bytes", [P, S], U8)
         zero = tile("zero", [P, 1], F32)
@@ -147,9 +148,9 @@ def tile_picked_nerfvol_none_p_kernel(tc, x_words, x_scales, w1, w2, bg, w3, off
 
         bg_rows = bg.rearrange("(a t r) v -> t a r v", t=PACK, r=RUN)
         w3_rows = w3.rearrange("(a t r) m -> t a r m", t=PACK, r=RUN)
-        bg_all = placed("bg_all", [P, PACK, V], F32, BG_AT)
+        bg_t = [placed("bg%d" % t, [P, V], F32, at) for t, at in enumerate(BG_AT)]
         for t in range(PACK):
-            nc.sync.dma_start(bg_all[:, t, :], bg_rows[t])
+            nc.sync.dma_start(bg_t[t][:], bg_rows[t])
         w3_raw = placed("w3_raw", [P, PACK, N], F32, W3_AT)
         for t in range(PACK):
             nc.sync.dma_start(w3_raw[:, t, :], w3_rows[t])
@@ -181,14 +182,18 @@ def tile_picked_nerfvol_none_p_kernel(tc, x_words, x_scales, w1, w2, bg, w3, off
         m2 = [placed("m2_%d" % t, [P, V], F32, M2_AT + t) for t in range(PACK)]
 
         def far_product(t):
-            nc.vector.tensor_tensor(m2[t][:], e[t][:].indirect(p2_t[:]), bg_all[:, t, :], ALU.mult)
+            nc.vector.tensor_tensor(m2[t][:], e[t][:].indirect(p2_t[:]), bg_t[t][:], ALU.mult)
 
         def emission(t):
-            nc.vector.scalar_tensor_tensor(a[t][:], e[t][:], one[:], val_ps[t][:], ALU.subtract, ALU.mult)
+            nc.vector.scalar_tensor_tensor(a[t][:], e[t][:], 1.0, val_ps[t][:], ALU.subtract, ALU.mult)
 
         for t in range(PACK):
             for step in (far_product, emission) if t < PACK - 1 else (emission, far_product):
                 step(t)
+        w3_first = placed("w3_bf0", [P, P * PACK], BF16, W3_BF_AT[0])
+        nc.gpsimd.tensor_scalar(
+            w3_first[:].rearrange("p (c t) -> p c t", t=PACK), w3_raw[:, :, :P].rearrange("p t c -> p c t"), one[:], 0.0, ALU.mult, ALU.add
+        )
         a1, a2 = [placed("a%d_fetched" % (1 + n), [P, PACK, V], F32, at) for n, at in enumerate(FETCHED_AT)]
         for dst, list_t in ((a2, p2_t), (a1, p1_t)):
             for t in range(PACK):
@@ -205,11 +210,12 @@ def tile_picked_nerfvol_none_p_kernel(tc, x_words, x_scales, w1, w2, bg, w3, off
             nc.vector.tensor_tensor(m1[:, t, rays], e[t][:].indirect(p1_t[:, entries]), behind[:, t, rays], ALU.mult)
 
         far_blend(0)
-        w3_bf = [placed("w3_bf%d" % g, [P, N * PACK // 2], BF16, at) for g, at in enumerate(W3_BF_AT)]
+        w3_second = placed("w3_bf1", [P, P * PACK], BF16, W3_BF_AT[1])
+        w3_rest = placed("w3_bf2", [P, N * PACK // 2], BF16, W3_BF_AT[2])
         w3_sc = tiles("w3_sc", [P, N // 2], U8, 2)
-        nc.scalar.copy(*weave(w3_bf[0][:], w3_raw[:, :, : N // 2]))
+        nc.scalar.copy(*weave(w3_second[:], w3_raw[:, :, P : 2 * P]))
         for u in (2, 3):
-            nc.scalar.copy(*weave(w3_bf[1][:, halves(N * PACK // 2)[u % 2]], w3_raw[:, :, u * P : (u + 1) * P]))
+            nc.scalar.copy(*weave(w3_rest[:, halves(N * PACK // 2)[u % 2]], w3_raw[:, :, u * P : (u + 1) * P]))
         for t in range(1, PACK):
             far_blend(t)
             near_product(t - 1)
@@ -227,11 +233,11 @@ def tile_picked_nerfvol_none_p_kernel(tc, x_words, x_scales, w1, w2, bg, w3, off
         w3_codes = [placed("w3_codes%d" % g, [P, N // 2], U32, at) for g, at in enumerate(W3_CODES_AT)]
 
         quantise(z_codes[:, first], z_sc[:, first], z_halves[0])
-        quantise(w3_codes[0][:, :P], w3_sc[0][:, :P], w3_bf[0][:, : P * PACK])
+        quantise(w3_codes[0][:, :P], w3_sc[0][:, :P], w3_first[:])
         quantise(z_codes[:, second], z_sc[:, second], z_halves[1])
-        quantise(w3_codes[0][:, P:], w3_sc[0][:, P:], w3_bf[0][:, P * PACK :])
+        quantise(w3_codes[0][:, P:], w3_sc[0][:, P:], w3_second[:])
         for cols, rounded in zip(halves(N // 2), halves(N * PACK // 2)):
-            quantise(w3_codes[1][:, cols], w3_sc[1][:, cols], w3_bf[1][:, rounded])
+            quantise(w3_codes[1][:, cols], w3_sc[1][:, cols], w3_rest[:, rounded])
 
         out_rows = out.rearrange("(u p) v -> u p v", p=P)
 

@@ -195,9 +195,14 @@ def tile_picked_nerfvol_none_p_kernel(tc, x_words, x_scales, w1, w2, bg, w3, off
             w3_first[:].rearrange("p (c t) -> p c t", t=PACK), w3_raw[:, :, :P].rearrange("p t c -> p c t"), one[:], 0.0, ALU.mult, ALU.add
         )
         a1, a2 = [placed("a%d_fetched" % (1 + n), [P, PACK, V], F32, at) for n, at in enumerate(FETCHED_AT)]
-        for dst, list_t in ((a2, p2_t), (a1, p1_t)):
-            for t in range(PACK):
-                nc.scalar.activation(dst[:, t, :], a[t][:].indirect(list_t[:]), ACT.Copy)
+        for t in range(PACK):
+            nc.scalar.activation(a2[:, t, :], a[t][:].indirect(p2_t[:]), ACT.Copy)
+        e1_last = tile("e1_last", [P, V // 2], F32)
+        nc.scalar.activation(e1_last[:], e[PACK - 1][:].indirect(p1_t[:, halves(V // GROUP)[0]]), ACT.Copy)
+        for t in range(PACK - 1):
+            nc.scalar.activation(a1[:, t, :], a[t][:].indirect(p1_t[:]), ACT.Copy)
+        for rays, entries in zip(halves(V), halves(V // GROUP)):
+            nc.scalar.activation(a1[:, PACK - 1, rays], a[PACK - 1][:].indirect(p1_t[:, entries]), ACT.Copy)
 
         behind = tile("behind", [P, PACK, V], F32)
         m1 = placed("m1", [P, PACK, V], F32, M1_AT)
@@ -219,8 +224,8 @@ def tile_picked_nerfvol_none_p_kernel(tc, x_words, x_scales, w1, w2, bg, w3, off
         for t in range(1, PACK):
             far_blend(t)
             near_product(t - 1)
-        for rays, entries in zip(halves(V), halves(V // GROUP)):
-            near_product(PACK - 1, rays, entries)
+        nc.vector.tensor_tensor(m1[:, PACK - 1, first], e1_last[:], behind[:, PACK - 1, first], ALU.mult)
+        near_product(PACK - 1, second, halves(V // GROUP)[1])
 
         z_bf = tile("z_bf", [P, V * PACK], BF16)
         z_codes = tile("z_codes", [P, V], U32)

@@ -29,7 +29,7 @@ FETCHED_AT = (6, 48)
 E_AT = 20
 W3_CODES_AT = (26, 56)
 A_AT = 28
-W3_BF_AT = (5, 32, 34)
+W3_BF_AT = (5, 33.5, 34.5)
 M2_AT = 40
 M1_AT = 56
 
@@ -53,7 +53,7 @@ def tile_picked_nerfvol_none_p_kernel(tc, x_words, x_scales, w1, w2, bg, w3, off
             return [tile("%s%d" % (name, n), shape, dtype) for n in range(count)]
 
         def placed(name, shape, dtype, kib):
-            return shared.tile(shape, dtype, name=name, offset=kib * 1024, align_bytes=64)
+            return shared.tile(shape, dtype, name=name, offset=int(kib * 1024), align_bytes=64)
 
         def bank(n, columns):
             return ps.tile([P, columns], F32, name="bank%d" % n)
@@ -199,10 +199,11 @@ def tile_picked_nerfvol_none_p_kernel(tc, x_words, x_scales, w1, w2, bg, w3, off
             nc.scalar.activation(a2[:, t, :], a[t][:].indirect(p2_t[:]), ACT.Copy)
         e1_last = tile("e1_last", [P, V // 2], F32)
         nc.scalar.activation(e1_last[:], e[PACK - 1][:].indirect(p1_t[:, halves(V // GROUP)[0]]), ACT.Copy)
-        for t in range(PACK - 1):
+        for t in (0, 1):
             nc.scalar.activation(a1[:, t, :], a[t][:].indirect(p1_t[:]), ACT.Copy)
         for rays, entries in zip(halves(V), halves(V // GROUP)):
-            nc.scalar.activation(a1[:, PACK - 1, rays], a[PACK - 1][:].indirect(p1_t[:, entries]), ACT.Copy)
+            for t in (2, 3):
+                nc.scalar.activation(a1[:, t, rays], a[t][:].indirect(p1_t[:, entries]), ACT.Copy)
 
         behind = tile("behind", [P, PACK, V], F32)
         m1 = placed("m1", [P, PACK, V], F32, M1_AT)

@@ -29,7 +29,7 @@ FETCHED_AT = (6, 48)
 E_AT = 20
 W3_CODES_AT = (26, 56)
 A_AT = 28
-W3_BF_AT = (5, 33.5, 34.5)
+W3_BF_AT = (5, 32, 34)
 M2_AT = 40
 M1_AT = 56
 
@@ -53,7 +53,7 @@ def tile_picked_nerfvol_none_p_kernel(tc, x_words, x_scales, w1, w2, bg, w3, off
             return [tile("%s%d" % (name, n), shape, dtype) for n in range(count)]
 
         def placed(name, shape, dtype, kib):
-            return shared.tile(shape, dtype, name=name, offset=int(kib * 1024), align_bytes=64)
+            return shared.tile(shape, dtype, name=name, offset=kib * 1024, align_bytes=64)
 
         def bank(n, columns):
             return ps.tile([P, columns], F32, name="bank%d" % n)

from contextlib import ExitStack

import concourse.mybir as mybir

F32, BF16 = mybir.dt.float32, mybir.dt.bfloat16
I32, U32, U16, U8 = mybir.dt.int32, mybir.dt.uint32, mybir.dt.uint16, mybir.dt.uint8
FP8X4 = mybir.dt.float8_e4m3fn_x4
ALU = mybir.AluOpType
ACT = mybir.ActivationFunctionType

K, T, S, V, N, H = 512, 2048, 512, 256, 512, 512
P = 128
PACK = 4
RUN = 4
GROUP = 16
QUADRANT = 32
SCALE_ROWS = 4
SCALES_FROM = P - K // 32
FLOPS = 2 * (2 * K * H * S + H * N * V)

W1_AT = 2
W2_AT = (10, 14)
SCALES_AT = 13
BG_AT = (3, 4, 5, 6)
WORDS_AT = 60
W3_AT = 60
DENS_AT = (48, 50)
FETCHED_AT = (6, 48)
E_AT = 20
W3_CODES_AT = (26, 56)
A_AT = 28
W3_BF_AT = (5, 32, 34)
M2_AT = 40
M1_AT = 56


def halves(n):
    return slice(0, n // 2), slice(n // 2, n)


def tile_picked_nerfvol_none_p_kernel(tc, x_words, x_scales, w1, w2, bg, w3, offs, p1, p2, out):
    nc = tc.nc
    with ExitStack() as ctx:
        lists = ctx.enter_context(tc.tile_pool(name="lists", bufs=1))
        sb = ctx.enter_context(tc.tile_pool(name="sb", bufs=1))
        shared = ctx.enter_context(tc.tile_pool(name="shared", bufs=1))
        ps = ctx.enter_context(tc.psum_pool(name="ps", bufs=1))

        def tile(name, shape, dtype, tag=None):
            return sb.tile(shape, dtype, name=name, tag=tag or name, align_bytes=64)

        def tiles(name, shape, dtype, count=PACK):
            return [tile("%s%d" % (name, n), shape, dtype) for n in range(count)]

        def placed(name, shape, dtype, kib):
            return shared.tile(shape, dtype, name=name, offset=kib * 1024, align_bytes=64)

        def bank(n, columns):
            return ps.tile([P, columns], F32, name="bank%d" % n)

        def weave(dst, src):
            return dst.rearrange("p (c i t) -> p c t i", i=RUN, t=PACK), src.rearrange("p t (c i) -> p c t i", i=RUN)

        def quantise(codes, scale_bytes, rounded):
            nc.vector.quantize_mx(out=codes.bitcast(FP8X4), scales=scale_bytes, in_=rounded)

        def multiply(dst, lhs_codes, lhs_scales, rhs_codes, rhs_scales):
            nc.tensor.matmul_mx(
                out=dst,
                lhsT=lhs_codes.bitcast(FP8X4),
                lhsT_scale=lhs_scales,
                rhs=rhs_codes.bitcast(FP8X4),
                rhs_scale=rhs_scales,
                start=True,
                stop=True,
            )

        offs_t = lists.tile([P, S // GROUP], U16, name="offs_t")
        p1_t = lists.tile([P, V // GROUP], U16, name="p1_t")
        p2_t = lists.tile([P, V // GROUP], U16, name="p2_t")
        words = placed("words", [P, T], U32, WORDS_AT)
        scales = placed("scales", [P, T], U8, SCALES_AT)
        x_bytes = tile("x_bytes", [P, S], U8)
        zero = tile("zero", [P, 1], F32)
        one = tile("one", [P, 1], F32)

        nc.vector.memset(zero[:], 0.0)
        nc.vector.memset(scales[:SCALES_FROM, :].bitcast(I32), 0)
        nc.vector.memset(x_bytes[:].bitcast(I32), 0)
        w1_raw = placed("w1_raw", [P, PACK, H], F32, W1_AT)
        nc.sync.dma_start(offs_t[:], offs)
        nc.scalar.dma_start(scales[SCALES_FROM:, :].bitcast(I32), x_scales[0].bitcast(I32))
        nc.sync.dma_start(w1_raw[:], w1.rearrange("(p j) c -> p j c", j=PACK))
        nc.sync.dma_start(p2_t[:], p2)
        nc.sync.dma_start(words[:].bitcast(I32), x_words[0].rearrange("p n j -> p (n j)").bitcast(I32))
        nc.sync.dma_start(p1_t[:], p1)
        nc.scalar.activation(one[:], zero[:], ACT.Exp)

        picked_scales = tile("picked_scales", [P, S], U8)
        x_codes = tiles("x_codes", [P, S // 2], U32, 2)
        samples = halves(S)
        nc.vector.tensor_copy(picked_scales[:], scales[:].indirect(offs_t[:]))
        for quadrant in range(P // QUADRANT):
            src = SCALES_FROM + SCALE_ROWS * quadrant
            dst = QUADRANT * quadrant
            nc.sync.dma_start(
                x_bytes[dst : dst + SCALE_ROWS, :].bitcast(I32), picked_scales[src : src + SCALE_ROWS, :].bitcast(I32)
            )
        w2_raw = [placed("w2_raw%d" % part, [P, PACK // 2, H], F32, at) for part, at in enumerate(W2_AT)]
        for part, js in enumerate(halves(PACK)):
            nc.sync.dma_start(w2_raw[part][:], w2.rearrange("(p j) c -> p j c", j=PACK)[:, js])

        def project(dst, codes, scale_bytes, h):
            multiply(dst, codes[:], scale_bytes[:], x_codes[h][:], x_bytes[:, samples[h]])

        def rounding_views(dst, raw, t0, t1):
            return (
                dst.rearrange("p (t a r j) -> p a t j r", t=t1 - t0, r=RUN, j=PACK),
                raw.rearrange("p j (a t r) -> p a t j r", t=PACK, r=RUN)[:, :, t0:t1],
            )

        w1_bf = tiles("w1_bf", [P, H], BF16)
        w1_codes = tiles("w1_codes", [P, P], U32)
        w1_sc = tiles("w1_sc", [P, P], U8)
        for t in range(PACK):
            (nc.vector.tensor_copy, nc.scalar.copy)[t % 2](*rounding_views(w1_bf[t][:], w1_raw[:], t, t + 1))
        for t in range(PACK):
            quantise(w1_codes[t][:], w1_sc[t][:], w1_bf[t][:])
        for h in range(2):
            nc.vector.tensor_copy(x_codes[h][:], words[:].indirect(offs_t[:, halves(S // GROUP)[h]]))
        e = [placed("e%d" % t, [P, S], F32, E_AT + 2 * t) for t in range(PACK)]
        dens = [placed("dens%d" % t, [P, S], F32, DENS_AT[t]) for t in range(2)]
        for h, cols in enumerate(samples):
            for t in range(2):
                acc = bank(2 * h + t, S // 2)
                project(acc[:], w1_codes[t], w1_sc[t], h)
                nc.scalar.activation(dens[t][:, cols], acc[:], ACT.Relu)
        for t in range(2):
            nc.scalar.activation(e[t][:], dens[t][:], ACT.Exp, scale=-1.0)
        dens = [placed("dens%d" % (2 + t), [P, S], F32, DENS_AT[t]) for t in range(2)]
        for t in range(2):
            acc = bank(4 + t, S)
            for h, cols in enumerate(samples):
                project(acc[:, cols], w1_codes[2 + t], w1_sc[2 + t], h)
            nc.scalar.activation(dens[t][:], acc[:], ACT.Relu)
        for t in range(2):
            nc.scalar.activation(e[2 + t][:], dens[t][:], ACT.Exp, scale=-1.0)

        bg_rows = bg.rearrange("(a t r) v -> t a r v", t=PACK, r=RUN)
        w3_rows = w3.rearrange("(a t r) m -> t a r m", t=PACK, r=RUN)
        bg_t = [placed("bg%d" % t, [P, V], F32, at) for t, at in enumerate(BG_AT)]
        for t in range(PACK):
            nc.sync.dma_start(bg_t[t][:], bg_rows[t])
        w3_raw = placed("w3_raw", [P, PACK, N], F32, W3_AT)
        for t in range(PACK):
            nc.sync.dma_start(w3_raw[:, t, :], w3_rows[t])

        w2_codes = tiles("w2_codes", [P, P], U32)
        w2_sc = tiles("w2_sc", [P, P], U8)
        spans = ((0, 1), (1, 2), (2, 4))
        w2_bf = [tile("w2_bf%d" % t0, [P, (t1 - t0) * H], BF16) for t0, t1 in spans]

        def w2_round(span, part):
            dst, src = rounding_views(w2_bf[span][:], w2_raw[part][:], *spans[span])
            nc.vector.tensor_copy(dst[:, :, :, halves(PACK)[part]], src)

        for span in range(len(spans)):
            w2_round(span, 0)
        w2_round(0, 1)
        w2_round(1, 1)
        quantise(w2_codes[0][:], w2_sc[0][:], w2_bf[0][:])
        w2_round(2, 1)
        quantise(w2_codes[1][:], w2_sc[1][:], w2_bf[1][:])
        for t in (2, 3):
            quantise(w2_codes[t][:], w2_sc[t][:], w2_bf[2][:, (t - 2) * H : (t - 1) * H])
        val_ps = [bank((6 + t) % 8, S) for t in range(PACK)]
        for t in range(PACK):
            for h, cols in enumerate(samples):
                project(val_ps[t][:, cols], w2_codes[t], w2_sc[t], h)

        a = [placed("a%d" % t, [P, S], F32, A_AT + 2 * t) for t in range(PACK)]
        m2 = [placed("m2_%d" % t, [P, V], F32, M2_AT + t) for t in range(PACK)]

        def far_product(t):
            nc.vector.tensor_tensor(m2[t][:], e[t][:].indirect(p2_t[:]), bg_t[t][:], ALU.mult)

        def emission(t):
            nc.vector.scalar_tensor_tensor(a[t][:], e[t][:], 1.0, val_ps[t][:], ALU.subtract, ALU.mult)

        for t in range(PACK):
            for step in (far_product, emission) if t < PACK - 1 else (emission, far_product):
                step(t)
        w3_first = placed("w3_bf0", [P, P * PACK], BF16, W3_BF_AT[0])
        nc.gpsimd.tensor_scalar(
            w3_first[:].rearrange("p (c t) -> p c t", t=PACK), w3_raw[:, :, :P].rearrange("p t c -> p c t"), one[:], 0.0, ALU.mult, ALU.add
        )
        a1, a2 = [placed("a%d_fetched" % (1 + n), [P, PACK, V], F32, at) for n, at in enumerate(FETCHED_AT)]
        for t in range(PACK):
            nc.scalar.activation(a2[:, t, :], a[t][:].indirect(p2_t[:]), ACT.Copy)
        e1_last = tile("e1_last", [P, V // 2], F32)
        nc.scalar.activation(e1_last[:], e[PACK - 1][:].indirect(p1_t[:, halves(V // GROUP)[0]]), ACT.Copy)
        for t in (0, 1):
            nc.scalar.activation(a1[:, t, :], a[t][:].indirect(p1_t[:]), ACT.Copy)
        for rays, entries in zip(halves(V), halves(V // GROUP)):
            for t in (2, 3):
                nc.scalar.activation(a1[:, t, rays], a[t][:].indirect(p1_t[:, entries]), ACT.Copy)

        behind = tile("behind", [P, PACK, V], F32)
        m1 = placed("m1", [P, PACK, V], F32, M1_AT)
        first, second = halves(V)

        def far_blend(t):
            nc.vector.tensor_tensor(behind[:, t, :], m2[t][:], a2[:, t, :], ALU.subtract)

        def near_product(t, rays=slice(0, V), entries=slice(0, V // GROUP)):
            nc.vector.tensor_tensor(m1[:, t, rays], e[t][:].indirect(p1_t[:, entries]), behind[:, t, rays], ALU.mult)

        far_blend(0)
        w3_second = placed("w3_bf1", [P, P * PACK], BF16, W3_BF_AT[1])
        w3_rest = placed("w3_bf2", [P, N * PACK // 2], BF16, W3_BF_AT[2])
        w3_sc = tiles("w3_sc", [P, N // 2], U8, 2)
        nc.scalar.copy(*weave(w3_second[:], w3_raw[:, :, P : 2 * P]))
        for u in (2, 3):
            nc.scalar.copy(*weave(w3_rest[:, halves(N * PACK // 2)[u % 2]], w3_raw[:, :, u * P : (u + 1) * P]))
        for t in range(1, PACK):
            far_blend(t)
            near_product(t - 1)
        nc.vector.tensor_tensor(m1[:, PACK - 1, first], e1_last[:], behind[:, PACK - 1, first], ALU.mult)
        near_product(PACK - 1, second, halves(V // GROUP)[1])

        z_bf = tile("z_bf", [P, V * PACK], BF16)
        z_codes = tile("z_codes", [P, V], U32)
        z_sc = tile("z_sc", [P, V], U8)
        z_halves = [z_bf[:, cols] for cols in halves(V * PACK)]
        for z_half, rays in zip(z_halves, (first, second)):
            z_view, m1_view = weave(z_half, m1[:, :, rays])
            z_view, a1_view = weave(z_half, a1[:, :, rays])
            nc.vector.tensor_tensor(z_view, m1_view, a1_view, ALU.subtract)
        w3_codes = [placed("w3_codes%d" % g, [P, N // 2], U32, at) for g, at in enumerate(W3_CODES_AT)]

        quantise(z_codes[:, first], z_sc[:, first], z_halves[0])
        quantise(w3_codes[0][:, :P], w3_sc[0][:, :P], w3_first[:])
        quantise(z_codes[:, second], z_sc[:, second], z_halves[1])
        quantise(w3_codes[0][:, P:], w3_sc[0][:, P:], w3_second[:])
        for cols, rounded in zip(halves(N // 2), halves(N * PACK // 2)):
            quantise(w3_codes[1][:, cols], w3_sc[1][:, cols], w3_rest[:, rounded])

        out_rows = out.rearrange("(u p) v -> u p v", p=P)

        def product(dst, u, rays):
            cols = halves(N // 2)[u % 2]
            multiply(dst, w3_codes[u // 2][:, cols], w3_sc[u // 2][:, cols], z_codes[:, rays], z_sc[:, rays])

        for u in range(PACK):
            res = tile("res%d" % u, [P, V], F32)
            empty = (nc.scalar.copy, nc.vector.tensor_copy)[u % 2]
            if u in (0, PACK - 1):
                for h, rays in enumerate((first, second)):
                    acc = bank(2 + h if u == 0 else 6 + h, V // 2)
                    product(acc[:], u, rays)
                    empty(res[:, rays], acc[:])
            else:
                acc = bank(3 + u, V)
                product(acc[:], u, slice(0, V))
                empty(res[:], acc[:])
            nc.sync.dma_start(out_rows[u], res[:])
